import numpy as np
import ml_dtypes


def mxq(x, axis, fmt="e4m3"):
    dtype, down = {"e4m3": (ml_dtypes.float8_e4m3fn, 7), "e5m2": (ml_dtypes.float8_e5m2, 14)}[fmt]
    v = np.moveaxis(np.asarray(x, np.float32).astype(ml_dtypes.bfloat16).astype(np.float64), axis, -1)
    blocks = v.reshape(v.shape[:-1] + (-1, 32))
    amax = np.abs(blocks).max(-1, keepdims=True)
    byte = np.maximum(np.where(amax > 0, np.frexp(amax)[1] - 1 + 127, 0) - down, 1)
    scale = np.exp2(byte - 127.0)
    codes = (blocks / scale).astype(np.float32).astype(dtype).astype(np.float64)
    return np.moveaxis((codes * scale).reshape(v.shape), -1, axis)


WIDE = False


def mx_kscale(k):
    if not WIDE:
        return np.ones(k)
    levels = np.array([10, -10, 5, -5, 0])
    if k % 512:
        return np.exp2(np.random.permutation(np.resize(levels, k // 32))).repeat(32)
    a = np.empty((k // 512, 16))
    for p in range(k // 512):
        a[p, :8] = np.random.permutation(np.resize(levels, 8))
        for g in range(8):
            far = levels[np.abs(levels - a[p, g]) >= 10]
            a[p, g + 8] = far[np.random.randint(len(far))]
    return np.exp2(a.ravel()).repeat(32)


def f64(x):
    return np.asarray(x).astype(np.float64)


def striped(idx):
    return np.tile(idx.reshape(-1, 16).T, (8, 1)).astype(np.uint16)


def unstriped(offs):
    return offs[:16].T.reshape(-1).astype(np.int64)


E2M1 = np.array([0.0, 0.5, 1.0, 1.5, 2.0, 3.0, 4.0, 6.0, -0.0, -0.5, -1.0, -1.5, -2.0, -3.0, -4.0, -6.0])


def pack_weight(w, fmt):
    k, n = w.shape
    w = f64(np.asarray(w, np.float32).astype(ml_dtypes.bfloat16)).reshape(k // 32, 32, n)
    amax = np.abs(w).max(1)
    if fmt == "e4m3":
        byte = np.frexp(amax)[1] - 1 + 127 - 7
    else:
        mant, ex = np.frexp(amax / 6.0)
        byte = np.where(mant > 0.5, ex, ex - 1) + 127
    byte = np.clip(np.where(amax > 0, byte, 1), 1, 254)
    scaled = (w * np.exp2(127.0 - byte)[:, None, :]).reshape(k, n).astype(np.float32)
    by_word = np.ascontiguousarray(scaled.reshape(k // 512, 128, 4, n).transpose(0, 1, 3, 2))
    if fmt == "e4m3":
        words = by_word.astype(ml_dtypes.float8_e4m3fn).view(np.uint8)
    else:
        c = by_word.astype(ml_dtypes.float4_e2m1fn).view(np.uint8) & 0xF
        words = (c[..., 0::2] | (c[..., 1::2] << 4)).reshape(k // 512, 128, 2 * n)
    return np.ascontiguousarray(words), np.ascontiguousarray(byte.astype(np.uint8).reshape(k // 512, 16, n))


def unpack_weight(words, scales, fmt):
    g, _, n = scales.shape
    words = np.ascontiguousarray(words).reshape(g, 128, n, -1)
    if fmt == "e4m3":
        vals = words.view(ml_dtypes.float8_e4m3fn).astype(np.float64)
    else:
        nib = np.empty((g, 128, n, 4), np.uint8)
        nib[..., 0::2] = words & 0xF
        nib[..., 1::2] = words >> 4
        vals = E2M1[nib]
    vals = vals * np.repeat(np.exp2(scales.astype(np.float64) - 127.0), 8, axis=1)[..., None]
    return vals.transpose(0, 1, 3, 2).reshape(g * 512, n)


def gelu(v):
    return 0.5 * v * (1.0 + np.tanh(np.sqrt(2.0 / np.pi) * (v + 0.044715 * v**3)))


def striped8(idx):
    return np.concatenate([v.reshape(-1, 16).T for v in idx]).astype(np.uint16)


def unstriped8(offs):
    return np.stack([offs[16 * g:16 * g + 16].T.reshape(-1) for g in range(8)]).astype(np.int64)


def runs(v, idx8):
    k = np.arange(v.shape[0])
    return v[k[:, None], idx8[k % 512 // 64]]


def put_heads(h, wgs, idx8, t2):
    r = np.arange(h.shape[0])
    page = np.zeros((h.shape[0], t2))
    page[r[:, None], idx8[r % 512 // 64]] = wgs[r // 4 % 128] * h
    return page


def often(T, S):
    return np.random.permutation(T)[(T * np.random.uniform(0, 1, S) ** 4).astype(np.int64)]


K, H, N, T, S, T2 = 512, 1024, 512, 2048, 1024, 2048

def setup_inputs():
    n = np.random.standard_normal
    s = mx_kscale(K)[:, None]
    u = mx_kscale(H)[:, None]
    tab_words, tab_scales = pack_weight(n((K, T)) * s, "e4m3")
    wa4_words, wa4_scales = pack_weight(n((K, H)) / np.sqrt(K) / s * u.T, "e2m1")
    wc8_words, wc8_scales = pack_weight(n((H, N)) / np.sqrt(H) / u, "e4m3")
    return {
        "tab_words": tab_words, "tab_scales": tab_scales,
        "offs": striped8(np.stack([often(T, S) for _ in range(8)])),
        "wa4_words": wa4_words, "wa4_scales": wa4_scales,
        "wb": (n((K, H)) / np.sqrt(K) / s * u.T).astype(np.float32),
        "wc8_words": wc8_words, "wc8_scales": wc8_scales,
        "wd": (n((H, N)) / np.sqrt(H) / u).astype(np.float32),
        "bd": (0.5 * n(N)).astype(np.float32),
        "wgo": np.repeat(np.random.uniform(0.5, 2.0, (8, S)), 16, axis=0).astype(np.float32),
        "offs2": striped8(np.stack([np.random.permutation(T2)[:S] for _ in range(8)])),
    }

def reference(tab_words, tab_scales, offs, wa4_words, wa4_scales, wb, wc8_words, wc8_scales, wd, bd, wgo, offs2):
    v = runs(unpack_weight(tab_words, tab_scales, "e4m3"), unstriped8(offs))
    ha = unpack_weight(wa4_words, wa4_scales, "e2m1").T @ v
    hb = mxq(f64(wb), 0, "e4m3").T @ v
    h = np.maximum(ha, hb)
    hq = mxq(h, 0, "e4m3")
    yc = unpack_weight(wc8_words, wc8_scales, "e4m3").T @ hq
    yd = mxq(f64(wd), 0, "e4m3").T @ hq
    gate = 1.0 / (1.0 + np.exp(-(yd + f64(bd)[:, None])))
    y = yc * gate
    out = put_heads(y, f64(wgo), unstriped8(offs2), T2)
    return out

@@ -1,0 +1,238 @@
+from contextlib import ExitStack
+
+import concourse.mybir as mybir
+
+K, H, N, T, S, T2 = 512, 1024, 512, 2048, 1024, 2048
+FLOPS = 4 * K * H * S + 4 * H * N * S
+
+F32 = mybir.dt.float32
+BF16 = mybir.dt.bfloat16
+I32 = mybir.dt.int32
+U32 = mybir.dt.uint32
+U16 = mybir.dt.uint16
+U8 = mybir.dt.uint8
+FP8X4 = mybir.dt.float8_e4m3fn_x4
+FP4X4 = mybir.dt.float4_e2m1fn_x4
+ALU = mybir.AluOpType
+ACT = mybir.ActivationFunctionType
+
+P = 128
+SLICES = [(0, 256), (256, 256), (512, 512)]
+
+
+def tile_list_profile_field_refresh_kernel(
+    tc, tab_words, tab_scales, offs, wa4_words, wa4_scales, wb, wc8_words, wc8_scales, wd, bd, wgo, offs2, out
+):
+    nc = tc.nc
+    with ExitStack() as ctx:
+        keep = ctx.enter_context(tc.tile_pool(name="keep", bufs=1))
+        ring = ctx.enter_context(tc.tile_pool(name="ring", bufs=2))
+        ps1 = ctx.enter_context(tc.psum_pool(name="ps1", bufs=4))
+        ps2 = ctx.enter_context(tc.psum_pool(name="ps2", bufs=4))
+
+        def held(name, shape, dtype):
+            return keep.tile(shape, dtype, name=name, align_bytes=64)
+
+        gather_list = keep.tile([P, S // 16], U16, name="gather_list")
+        scatter_list = keep.tile([P, S // 16], U16, name="scatter_list")
+
+        warm = keep.tile([P, 8], F32, name="warm", tag="page2", align_bytes=64)
+        warm_out = keep.tile([P, 8], F32, name="warm_out", tag="page3", align_bytes=64)
+        nc.vector.memset(warm[:], 0.0)
+        nc.scalar.activation(warm_out[:], warm[:], ACT.Sigmoid)
+
+        def shared(name, shape, dtype, tag):
+            return keep.tile(shape, dtype, name=name, tag=tag, align_bytes=64)
+
+        tab_s = held("tab_s", [P, T], U8)
+        w_s_raw = held("w_s_raw", [P, H], U8)
+        planes = held("planes", [P, H + S], U8)
+        nc.vector.memset(planes[:].bitcast(I32), 0)
+        wc8_s = held("wc8_s", [P, H], U8)
+        nc.vector.memset(wc8_s[:].bitcast(I32), 0)
+        w_s = planes[:, 0:H]
+        v_s = planes[:, H : H + S]
+
+        nc.sync.dma_start(gather_list[:], offs)
+        wb_rows = wb.rearrange("(p j) c -> p j c", j=4)
+        wb_raw = [shared("wb_raw%d" % b, [P, 4, 512], F32, "raw%d" % b) for b in range(2)]
+        nc.sync.dma_start(tab_s[:].bitcast(I32), tab_scales[0].bitcast(I32).unsqueeze(1).to_broadcast([16, 8, T // 4]))
+        nc.sync.dma_start(
+            w_s_raw[0:P:2, :].bitcast(I32), wa4_scales[0].bitcast(I32).unsqueeze(1).to_broadcast([16, 4, H // 4])
+        )
+        for a in range(2):
+            nc.sync.dma_start(
+                w_s_raw[1:P:2, N * a : N * (a + 1)].bitcast(I32),
+                wc8_scales[a].bitcast(I32).unsqueeze(1).to_broadcast([16, 4, N // 4]),
+            )
+        tab_w = held("tab_w", [P, T], U32)
+        nc.sync.dma_start(tab_w[:].bitcast(I32), tab_words[0].rearrange("p t i -> p (t i)").bitcast(I32))
+        wa4_raw = held("wa4_raw", [P, 2 * H], U8)
+        nc.sync.dma_start(wa4_raw[:].bitcast(I32), wa4_words[0].bitcast(I32))
+        nc.sync.dma_start(wb_raw[0][:], wb_rows[:, :, 0:512])
+        nc.sync.dma_start(wb_raw[1][:], wb_rows[:, :, 512:1024])
+        bias = held("bias", [P, 4], F32)
+        nc.sync.dma_start(bias[:], bd.rearrange("(p i) -> p i", i=4))
+        nc.sync.dma_start(scatter_list[:], offs2)
+        wd_raw = [held("wd_raw0", [P, 4, N], F32)]
+        nc.sync.dma_start(wd_raw[0][:], wd[0:512, :].rearrange("(p j) c -> p j c", j=4))
+
+        v_s_g = held("v_s_g", [P, S], U8)
+        nc.vector.tensor_copy(v_s_g[:], tab_s[:].indirect(gather_list[:]))
+        staged = held("staged", [P, H + S], U8)
+        nc.vector.tensor_copy(staged[:, H : H + S].bitcast(I32), v_s_g[:].bitcast(I32))
+        nc.vector.tensor_copy(
+            staged[:, 0:H].rearrange("p (b t m) -> p b t m", b=2, t=4),
+            w_s_raw[:].rearrange("p (b m t) -> p b t m", b=2, t=4),
+        )
+        for r in range(4):
+            nc.sync.dma_start(planes[r:P:32, :].bitcast(I32), staged[8 * r : P : 32, :].bitcast(I32))
+
+        v_w = []
+        for s, (j0, n) in enumerate(SLICES):
+            words = held("v_w%d" % s, [P, n], U32)
+            nc.vector.tensor_copy(words[:], tab_w[:].indirect(gather_list[:, j0 // 16 : (j0 + n) // 16]))
+            v_w.append(words)
+
+        wa4 = held("wa4", [P, 2 * H], U8)
+        nc.vector.tensor_copy(
+            wa4[:].bitcast(U16).rearrange("p (b t m) -> p b t m", b=2, t=4),
+            wa4_raw[:].bitcast(U16).rearrange("p (b m t) -> p b t m", b=2, t=4),
+        )
+
+        def cast_weight(copy, raw, name):
+            woven = shared(name, [P, 2048], BF16, name)
+            copy(woven[:].rearrange("p (t m j) -> p m t j", t=4, j=4), raw[:].rearrange("p j (m t) -> p m t j", t=4))
+            return woven
+
+        def quantise(woven, width, name):
+            codes = held(name + "_w", [P, width], U32)
+            scales = held(name + "_s", [P, width], U8)
+            nc.vector.quantize_mx(out=codes[:].bitcast(FP8X4), scales=scales[:], in_=woven[:])
+            return codes, scales
+
+        wbq = []
+        for b in range(2):
+            wbq.append(quantise(cast_weight([nc.scalar.copy, nc.vector.tensor_copy][b], wb_raw[b], "wb_bf%d" % b), 512, "wbq%d" % b))
+
+        wd_raw.append(shared("wd_raw1", [P, 4, N], F32, "raw0"))
+        nc.sync.dma_start(wd_raw[1][:], wd[512:1024, :].rearrange("(p j) c -> p j c", j=4))
+        wc8_raw = shared("wc8_raw", [P, 2, N], I32, "wb_bf0")
+        nc.sync.dma_start(wc8_raw[:], wc8_words.rearrange("a p c i -> p a (c i)").bitcast(I32))
+        wgo_sb = shared("wgo_sb", [P, S], F32, "raw1")
+        nc.sync.dma_start(wgo_sb[:], wgo)
+        for r in range(4):
+            nc.sync.dma_start(wc8_s[r:P:32, :].bitcast(I32), staged[8 * r + 1 : P : 32, 0:H].bitcast(I32))
+
+        def stage1(s):
+            j0, n = SLICES[s]
+            result = []
+            for b in range(2):
+                h = ring.tile([P, 4 * n], BF16, name="h", tag="h", align_bytes=64)
+                ha = ring.tile([P, 4 * n], F32 if s == 0 else BF16, name="ha", tag="ha", align_bytes=64)
+                if s > 0:
+                    hb = ring.tile([P, 4 * n], BF16, name="hb", tag="hb", align_bytes=64)
+                for c in range(n // P):
+                    rhs = v_w[s][:, c * P : (c + 1) * P].bitcast(FP8X4)
+                    rhs_scale = v_s[:, j0 + c * P : j0 + (c + 1) * P]
+                    bank_a = ps1.tile([P, 4, P], F32, name="bank_a", tag="bank")
+                    for t in range(4):
+                        col = 512 * b + P * t
+                        nc.tensor.matmul_mx(
+                            out=bank_a[:, t, :],
+                            lhsT=wa4[:, 2 * col : 2 * (col + P)].bitcast(FP4X4),
+                            lhsT_scale=w_s[:, col : col + P],
+                            rhs=rhs,
+                            rhs_scale=rhs_scale,
+                            start=True,
+                            stop=True,
+                        )
+                    nc.scalar.copy(
+                        ha[:, 512 * c : 512 * (c + 1)].rearrange("p (n t) -> p n t", t=4),
+                        bank_a[:].rearrange("p t n -> p n t"),
+                    )
+                    bank_b = ps1.tile([P, 4, P], F32, name="bank_b", tag="bank")
+                    for t in range(4):
+                        nc.tensor.matmul_mx(
+                            out=bank_b[:, t, :],
+                            lhsT=wbq[b][0][:, P * t : P * (t + 1)].bitcast(FP8X4),
+                            lhsT_scale=wbq[b][1][:, P * t : P * (t + 1)],
+                            rhs=rhs,
+                            rhs_scale=rhs_scale,
+                            start=True,
+                            stop=True,
+                        )
+                    if s == 0:
+                        nc.vector.tensor_tensor(
+                            h[:, 512 * c : 512 * (c + 1)].rearrange("p (n t) -> p n t", t=4),
+                            bank_b[:].rearrange("p t n -> p n t"),
+                            ha[:, 512 * c : 512 * (c + 1)].rearrange("p (n t) -> p n t", t=4),
+                            ALU.max,
+                        )
+                    else:
+                        nc.scalar.copy(
+                            hb[:, 512 * c : 512 * (c + 1)].rearrange("p (n t) -> p n t", t=4),
+                            bank_b[:].rearrange("p t n -> p n t"),
+                        )
+                if s > 0:
+                    nc.vector.tensor_tensor(h[:], ha[:], hb[:], ALU.max)
+                result.append(quantise(h, n, "hq%d_%d" % (s, b)))
+            return result
+
+        hq = [stage1(0)]
+
+        wdq = []
+        for a in range(2):
+            wdq.append(quantise(cast_weight([nc.scalar.copy, nc.vector.tensor_copy][a], wd_raw[a], "wd_bf%d" % a), 512, "wdq%d" % a))
+        wc8 = held("wc8", [P, 2 * N], U32)
+        nc.vector.tensor_copy(
+            wc8[:].rearrange("p (a i g m) -> p a g i m", a=2, i=4, m=4),
+            wc8_raw[:].bitcast(U32).rearrange("p a (g m i) -> p a g i m", i=4, m=4),
+        )
+
+        pages = [shared("page%d" % i, [P, T2], F32, "page%d" % i) for i in range(4)]
+        for i in range(4):
+            [nc.vector, nc.gpsimd][i // 2].memset(pages[i][:], 0.0)
+
+        out_rows = out.rearrange("(p i) t -> p i t", i=4)
+
+        def stage2(s, i):
+            j0, n = SLICES[s]
+            yd = ps2.tile([P, n], F32, name="yd", tag="y")
+            for a in range(2):
+                nc.tensor.matmul_mx(
+                    out=yd[:],
+                    lhsT=wdq[a][0][:, P * i : P * (i + 1)].bitcast(FP8X4),
+                    lhsT_scale=wdq[a][1][:, P * i : P * (i + 1)],
+                    rhs=hq[s][a][0][:].bitcast(FP8X4),
+                    rhs_scale=hq[s][a][1][:],
+                    start=(a == 0),
+                    stop=(a == 1),
+                )
+            yc = ps2.tile([P, n], F32, name="yc", tag="y")
+            for a in range(2):
+                col = N * a + P * i
+                nc.tensor.matmul_mx(
+                    out=yc[:],
+                    lhsT=wc8[:, col : col + P].bitcast(FP8X4),
+                    lhsT_scale=wc8_s[:, col : col + P],
+                    rhs=hq[s][a][0][:].bitcast(FP8X4),
+                    rhs_scale=hq[s][a][1][:],
+                    start=(a == 0),
+                    stop=(a == 1),
+                )
+            gate = ring.tile([P, n], F32, name="gate", tag="gate")
+            nc.scalar.activation(gate[:], yd[:], ACT.Sigmoid, bias=bias[:, i : i + 1])
+            y = ring.tile([P, n], F32, name="y", tag="ysb")
+            nc.vector.tensor_tensor(y[:], yc[:], gate[:], ALU.mult)
+            nc.vector.tensor_tensor(
+                pages[i][:].indirect(scatter_list[:, j0 // 16 : (j0 + n) // 16]), y[:], wgo_sb[:, j0 : j0 + n], ALU.mult
+            )
+            if s == len(SLICES) - 1:
+                nc.sync.dma_start(out_rows[:, i, :], pages[i][:])
+
+        for s in range(len(SLICES)):
+            for i in range(4):
+                if i == 2 and s + 1 < len(SLICES):
+                    hq.append(stage1(s + 1))
+                stage2(s, i)

@@ -17,7 +17,7 @@ ALU = mybir.AluOpType
 ACT = mybir.ActivationFunctionType
 
 P = 128
-SLICES = [(0, 256), (256, 256), (512, 512)]
+SLICES = [(0, 256), (256, 256), (512, 256), (768, 256)]
 
 
 def tile_list_profile_field_refresh_kernel(
@@ -27,6 +27,7 @@ def tile_list_profile_field_refresh_kernel(
     with ExitStack() as ctx:
         keep = ctx.enter_context(tc.tile_pool(name="keep", bufs=1))
         ring = ctx.enter_context(tc.tile_pool(name="ring", bufs=2))
+        ring3 = ctx.enter_context(tc.tile_pool(name="ring3", bufs=3))
         ps1 = ctx.enter_context(tc.psum_pool(name="ps1", bufs=4))
         ps2 = ctx.enter_context(tc.psum_pool(name="ps2", bufs=4))
 
@@ -48,8 +49,6 @@ def tile_list_profile_field_refresh_kernel(
         w_s_raw = held("w_s_raw", [P, H], U8)
         planes = held("planes", [P, H + S], U8)
         nc.vector.memset(planes[:].bitcast(I32), 0)
-        wc8_s = held("wc8_s", [P, H], U8)
-        nc.vector.memset(wc8_s[:].bitcast(I32), 0)
         w_s = planes[:, 0:H]
         v_s = planes[:, H : H + S]
 
@@ -65,15 +64,15 @@ def tile_list_profile_field_refresh_kernel(
                 w_s_raw[1:P:2, N * a : N * (a + 1)].bitcast(I32),
                 wc8_scales[a].bitcast(I32).unsqueeze(1).to_broadcast([16, 4, N // 4]),
             )
+        bias = held("bias", [P, 4], F32)
+        nc.sync.dma_start(bias[:], bd.rearrange("(p i) -> p i", i=4))
+        nc.sync.dma_start(scatter_list[:], offs2)
         tab_w = held("tab_w", [P, T], U32)
         nc.sync.dma_start(tab_w[:].bitcast(I32), tab_words[0].rearrange("p t i -> p (t i)").bitcast(I32))
         wa4_raw = held("wa4_raw", [P, 2 * H], U8)
         nc.sync.dma_start(wa4_raw[:].bitcast(I32), wa4_words[0].bitcast(I32))
         nc.sync.dma_start(wb_raw[0][:], wb_rows[:, :, 0:512])
         nc.sync.dma_start(wb_raw[1][:], wb_rows[:, :, 512:1024])
-        bias = held("bias", [P, 4], F32)
-        nc.sync.dma_start(bias[:], bd.rearrange("(p i) -> p i", i=4))
-        nc.sync.dma_start(scatter_list[:], offs2)
         wd_raw = [held("wd_raw0", [P, 4, N], F32)]
         nc.sync.dma_start(wd_raw[0][:], wd[0:512, :].rearrange("(p j) c -> p j c", j=4))
 
@@ -121,65 +120,66 @@ def tile_list_profile_field_refresh_kernel(
         nc.sync.dma_start(wc8_raw[:], wc8_words.rearrange("a p c i -> p a (c i)").bitcast(I32))
         wgo_sb = shared("wgo_sb", [P, S], F32, "raw1")
         nc.sync.dma_start(wgo_sb[:], wgo)
+        wc8_s = shared("wc8_s", [P, H], U8, "wb_bf1")
+        nc.vector.memset(wc8_s[:].bitcast(I32), 0)
         for r in range(4):
             nc.sync.dma_start(wc8_s[r:P:32, :].bitcast(I32), staged[8 * r + 1 : P : 32, 0:H].bitcast(I32))
 
-        def stage1(s):
+        def stage1(s, b):
             j0, n = SLICES[s]
-            result = []
-            for b in range(2):
-                h = ring.tile([P, 4 * n], BF16, name="h", tag="h", align_bytes=64)
-                ha = ring.tile([P, 4 * n], F32 if s == 0 else BF16, name="ha", tag="ha", align_bytes=64)
-                if s > 0:
-                    hb = ring.tile([P, 4 * n], BF16, name="hb", tag="hb", align_bytes=64)
-                for c in range(n // P):
-                    rhs = v_w[s][:, c * P : (c + 1) * P].bitcast(FP8X4)
-                    rhs_scale = v_s[:, j0 + c * P : j0 + (c + 1) * P]
-                    bank_a = ps1.tile([P, 4, P], F32, name="bank_a", tag="bank")
-                    for t in range(4):
-                        col = 512 * b + P * t
-                        nc.tensor.matmul_mx(
-                            out=bank_a[:, t, :],
-                            lhsT=wa4[:, 2 * col : 2 * (col + P)].bitcast(FP4X4),
-                            lhsT_scale=w_s[:, col : col + P],
-                            rhs=rhs,
-                            rhs_scale=rhs_scale,
-                            start=True,
-                            stop=True,
-                        )
-                    nc.scalar.copy(
-                        ha[:, 512 * c : 512 * (c + 1)].rearrange("p (n t) -> p n t", t=4),
-                        bank_a[:].rearrange("p t n -> p n t"),
+            h = ring.tile([P, 4 * n], BF16, name="h", tag="h", align_bytes=64)
+            ha = ring.tile([P, 4 * n], F32 if s == 0 else BF16, name="ha", tag="ha", align_bytes=64)
+            if s > 0:
+                hb = ring.tile([P, 4 * n], BF16, name="hb", tag="hb", align_bytes=64)
+            for c in range(n // P):
+                rhs = v_w[s][:, c * P : (c + 1) * P].bitcast(FP8X4)
+                rhs_scale = v_s[:, j0 + c * P : j0 + (c + 1) * P]
+                bank_a = ps1.tile([P, 4, P], F32, name="bank_a", tag="bank")
+                for t in range(4):
+                    col = 512 * b + P * t
+                    nc.tensor.matmul_mx(
+                        out=bank_a[:, t, :],
+                        lhsT=wa4[:, 2 * col : 2 * (col + P)].bitcast(FP4X4),
+                        lhsT_scale=w_s[:, col : col + P],
+                        rhs=rhs,
+                        rhs_scale=rhs_scale,
+                        start=True,
+                        stop=True,
                     )
-                    bank_b = ps1.tile([P, 4, P], F32, name="bank_b", tag="bank")
-                    for t in range(4):
-                        nc.tensor.matmul_mx(
-                            out=bank_b[:, t, :],
-                            lhsT=wbq[b][0][:, P * t : P * (t + 1)].bitcast(FP8X4),
-                            lhsT_scale=wbq[b][1][:, P * t : P * (t + 1)],
-                            rhs=rhs,
-                            rhs_scale=rhs_scale,
-                            start=True,
-                            stop=True,
-                        )
-                    if s == 0:
-                        nc.vector.tensor_tensor(
-                            h[:, 512 * c : 512 * (c + 1)].rearrange("p (n t) -> p n t", t=4),
-                            bank_b[:].rearrange("p t n -> p n t"),
-                            ha[:, 512 * c : 512 * (c + 1)].rearrange("p (n t) -> p n t", t=4),
-                            ALU.max,
-                        )
-                    else:
-                        nc.scalar.copy(
-                            hb[:, 512 * c : 512 * (c + 1)].rearrange("p (n t) -> p n t", t=4),
-                            bank_b[:].rearrange("p t n -> p n t"),
-                        )
-                if s > 0:
-                    nc.vector.tensor_tensor(h[:], ha[:], hb[:], ALU.max)
-                result.append(quantise(h, n, "hq%d_%d" % (s, b)))
-            return result
+                nc.scalar.copy(
+                    ha[:, 512 * c : 512 * (c + 1)].rearrange("p (n t) -> p n t", t=4),
+                    bank_a[:].rearrange("p t n -> p n t"),
+                )
+                bank_b = ps1.tile([P, 4, P], F32, name="bank_b", tag="bank")
+                for t in range(4):
+                    nc.tensor.matmul_mx(
+                        out=bank_b[:, t, :],
+                        lhsT=wbq[b][0][:, P * t : P * (t + 1)].bitcast(FP8X4),
+                        lhsT_scale=wbq[b][1][:, P * t : P * (t + 1)],
+                        rhs=rhs,
+                        rhs_scale=rhs_scale,
+                        start=True,
+                        stop=True,
+                    )
+                if s == 0:
+                    nc.vector.tensor_tensor(
+                        h[:, 512 * c : 512 * (c + 1)].rearrange("p (n t) -> p n t", t=4),
+                        bank_b[:].rearrange("p t n -> p n t"),
+                        ha[:, 512 * c : 512 * (c + 1)].rearrange("p (n t) -> p n t", t=4),
+                        ALU.max,
+                    )
+                else:
+                    nc.scalar.copy(
+                        hb[:, 512 * c : 512 * (c + 1)].rearrange("p (n t) -> p n t", t=4),
+                        bank_b[:].rearrange("p t n -> p n t"),
+                    )
+            if s > 0:
+                nc.vector.tensor_tensor(h[:], ha[:], hb[:], ALU.max)
+            hq[s, b] = quantise(h, n, "hq%d_%d" % (s, b))
 
-        hq = [stage1(0)]
+        hq = {}
+        stage1(0, 0)
+        stage1(0, 1)
 
         wdq = []
         for a in range(2):
@@ -204,8 +204,8 @@ def tile_list_profile_field_refresh_kernel(
                     out=yd[:],
                     lhsT=wdq[a][0][:, P * i : P * (i + 1)].bitcast(FP8X4),
                     lhsT_scale=wdq[a][1][:, P * i : P * (i + 1)],
-                    rhs=hq[s][a][0][:].bitcast(FP8X4),
-                    rhs_scale=hq[s][a][1][:],
+                    rhs=hq[s, a][0][:].bitcast(FP8X4),
+                    rhs_scale=hq[s, a][1][:],
                     start=(a == 0),
                     stop=(a == 1),
                 )
@@ -216,23 +216,33 @@ def tile_list_profile_field_refresh_kernel(
                     out=yc[:],
                     lhsT=wc8[:, col : col + P].bitcast(FP8X4),
                     lhsT_scale=wc8_s[:, col : col + P],
-                    rhs=hq[s][a][0][:].bitcast(FP8X4),
-                    rhs_scale=hq[s][a][1][:],
+                    rhs=hq[s, a][0][:].bitcast(FP8X4),
+                    rhs_scale=hq[s, a][1][:],
                     start=(a == 0),
                     stop=(a == 1),
                 )
             gate = ring.tile([P, n], F32, name="gate", tag="gate")
             nc.scalar.activation(gate[:], yd[:], ACT.Sigmoid, bias=bias[:, i : i + 1])
-            y = ring.tile([P, n], F32, name="y", tag="ysb")
-            nc.vector.tensor_tensor(y[:], yc[:], gate[:], ALU.mult)
-            nc.vector.tensor_tensor(
-                pages[i][:].indirect(scatter_list[:, j0 // 16 : (j0 + n) // 16]), y[:], wgo_sb[:, j0 : j0 + n], ALU.mult
-            )
+            y = ring3.tile([P, n], F32, name="y", tag="ysb")
+            places = pages[i][:].indirect(scatter_list[:, j0 // 16 : (j0 + n) // 16])
+            if (s, i) == (0, 0):
+                nc.vector.tensor_tensor(y[:], yc[:], gate[:], ALU.mult)
+                nc.vector.tensor_tensor(places, y[:], wgo_sb[:, j0 : j0 + n], ALU.mult)
+            else:
+                yc_sb = ring.tile([P, n], F32, name="yc_sb", tag="yc_sb")
+                nc.scalar.copy(yc_sb[:], yc[:])
+                gw = ring.tile([P, n], F32, name="gw", tag="gw")
+                for c in range(0, n, 256):
+                    nc.gpsimd.tensor_tensor(gw[:, c : c + 256], gate[:, c : c + 256], wgo_sb[:, j0 + c : j0 + c + 256], ALU.mult)
+                    nc.gpsimd.tensor_tensor(y[:, c : c + 256], gw[:, c : c + 256], yc_sb[:, c : c + 256], ALU.mult)
+                nc.vector.tensor_copy(places, y[:])
             if s == len(SLICES) - 1:
                 nc.sync.dma_start(out_rows[:, i, :], pages[i][:])
 
-        for s in range(len(SLICES)):
-            for i in range(4):
-                if i == 2 and s + 1 < len(SLICES):
-                    hq.append(stage1(s + 1))
-                stage2(s, i)
+        order = [(s, i) for s in range(2) for i in range(4)]
+        order = order + [(2, 0), (2, 1), (3, 0), (2, 2), (3, 1), (2, 3), (3, 2), (3, 3)]
+        halves = {0: (1, 0), 1: (1, 1), 3: (2, 0), 4: (2, 1), 6: (3, 0), 7: (3, 1)}
+        for step, (s, i) in enumerate(order):
+            stage2(s, i)
+            if step in halves:
+                stage1(*halves[step])

@@ -17,7 +17,7 @@ ALU = mybir.AluOpType
 ACT = mybir.ActivationFunctionType
 
 P = 128
-SLICES = [(0, 256), (256, 256), (512, 256), (768, 256)]
+SLICES = [(0, 256), (256, 256), (512, 512)]
 
 
 def tile_list_profile_field_refresh_kernel(
@@ -38,7 +38,7 @@ def tile_list_profile_field_refresh_kernel(
         scatter_list = keep.tile([P, S // 16], U16, name="scatter_list")
 
         warm = keep.tile([P, 8], F32, name="warm", tag="page2", align_bytes=64)
-        warm_out = keep.tile([P, 8], F32, name="warm_out", tag="page3", align_bytes=64)
+        warm_out = keep.tile([P, 8], F32, name="warm_out", align_bytes=64)
         nc.vector.memset(warm[:], 0.0)
         nc.scalar.activation(warm_out[:], warm[:], ACT.Sigmoid)
 
@@ -46,7 +46,7 @@ def tile_list_profile_field_refresh_kernel(
             return keep.tile(shape, dtype, name=name, tag=tag, align_bytes=64)
 
         tab_s = held("tab_s", [P, T], U8)
-        w_s_raw = held("w_s_raw", [P, H], U8)
+        w_s_raw = shared("w_s_raw", [P, H], U8, "w_s_raw")
         planes = held("planes", [P, H + S], U8)
         nc.vector.memset(planes[:].bitcast(I32), 0)
         w_s = planes[:, 0:H]
@@ -67,14 +67,12 @@ def tile_list_profile_field_refresh_kernel(
         bias = held("bias", [P, 4], F32)
         nc.sync.dma_start(bias[:], bd.rearrange("(p i) -> p i", i=4))
         nc.sync.dma_start(scatter_list[:], offs2)
-        tab_w = held("tab_w", [P, T], U32)
-        nc.sync.dma_start(tab_w[:].bitcast(I32), tab_words[0].rearrange("p t i -> p (t i)").bitcast(I32))
+        nc.sync.dma_start(wb_raw[0][:], wb_rows[:, :, 0:512])
         wa4_raw = held("wa4_raw", [P, 2 * H], U8)
         nc.sync.dma_start(wa4_raw[:].bitcast(I32), wa4_words[0].bitcast(I32))
-        nc.sync.dma_start(wb_raw[0][:], wb_rows[:, :, 0:512])
         nc.sync.dma_start(wb_raw[1][:], wb_rows[:, :, 512:1024])
-        wd_raw = [held("wd_raw0", [P, 4, N], F32)]
-        nc.sync.dma_start(wd_raw[0][:], wd[0:512, :].rearrange("(p j) c -> p j c", j=4))
+        tab_w = held("tab_w", [P, T], U32)
+        nc.sync.dma_start(tab_w[:].bitcast(I32), tab_words[0].rearrange("p t i -> p (t i)").bitcast(I32))
 
         v_s_g = held("v_s_g", [P, S], U8)
         nc.vector.tensor_copy(v_s_g[:], tab_s[:].indirect(gather_list[:]))
@@ -87,11 +85,8 @@ def tile_list_profile_field_refresh_kernel(
         for r in range(4):
             nc.sync.dma_start(planes[r:P:32, :].bitcast(I32), staged[8 * r : P : 32, :].bitcast(I32))
 
-        v_w = []
-        for s, (j0, n) in enumerate(SLICES):
-            words = held("v_w%d" % s, [P, n], U32)
-            nc.vector.tensor_copy(words[:], tab_w[:].indirect(gather_list[:, j0 // 16 : (j0 + n) // 16]))
-            v_w.append(words)
+        wd_raw = [shared("wd_raw0", [P, 4, N], F32, "w_s_raw")]
+        nc.sync.dma_start(wd_raw[0][:], wd[0:512, :].rearrange("(p j) c -> p j c", j=4))
 
         wa4 = held("wa4", [P, 2 * H], U8)
         nc.vector.tensor_copy(
@@ -99,10 +94,16 @@ def tile_list_profile_field_refresh_kernel(
             wa4_raw[:].bitcast(U16).rearrange("p (b m t) -> p b t m", b=2, t=4),
         )
 
-        def cast_weight(copy, raw, name):
+        def cast_weight(shares, raw, name):
             woven = shared(name, [P, 2048], BF16, name)
-            copy(woven[:].rearrange("p (t m j) -> p m t j", t=4, j=4), raw[:].rearrange("p j (m t) -> p m t j", t=4))
+            dst = woven[:].rearrange("p (t m j) -> p m t j", t=4, j=4)
+            src = raw[:].rearrange("p j (m t) -> p m t j", t=4)
+            for copy, m0, m1 in shares:
+                copy(dst[:, m0:m1], src[:, m0:m1])
             return woven
+
+        on_scalar = [(nc.scalar.copy, 0, P)]
+        on_both = [(nc.scalar.copy, 0, 64), (nc.vector.tensor_copy, 64, P)]
 
         def quantise(woven, width, name):
             codes = held(name + "_w", [P, width], U32)
@@ -112,7 +113,7 @@ def tile_list_profile_field_refresh_kernel(
 
         wbq = []
         for b in range(2):
-            wbq.append(quantise(cast_weight([nc.scalar.copy, nc.vector.tensor_copy][b], wb_raw[b], "wb_bf%d" % b), 512, "wbq%d" % b))
+            wbq.append(quantise(cast_weight(on_scalar, wb_raw[b], "wb_bf%d" % b), 512, "wbq%d" % b))
 
         wd_raw.append(shared("wd_raw1", [P, 4, N], F32, "raw0"))
         nc.sync.dma_start(wd_raw[1][:], wd[512:1024, :].rearrange("(p j) c -> p j c", j=4))
@@ -125,8 +126,17 @@ def tile_list_profile_field_refresh_kernel(
         for r in range(4):
             nc.sync.dma_start(wc8_s[r:P:32, :].bitcast(I32), staged[8 * r + 1 : P : 32, 0:H].bitcast(I32))
 
+        v_w = {}
+
+        def gather_words(s):
+            j0, n = SLICES[s]
+            v_w[s] = held("v_w%d" % s, [P, n], U32)
+            nc.vector.tensor_copy(v_w[s][:], tab_w[:].indirect(gather_list[:, j0 // 16 : (j0 + n) // 16]))
+
         def stage1(s, b):
             j0, n = SLICES[s]
+            if b == 0:
+                gather_words(s)
             h = ring.tile([P, 4 * n], BF16, name="h", tag="h", align_bytes=64)
             ha = ring.tile([P, 4 * n], F32 if s == 0 else BF16, name="ha", tag="ha", align_bytes=64)
             if s > 0:
@@ -183,14 +193,14 @@ def tile_list_profile_field_refresh_kernel(
 
         wdq = []
         for a in range(2):
-            wdq.append(quantise(cast_weight([nc.scalar.copy, nc.vector.tensor_copy][a], wd_raw[a], "wd_bf%d" % a), 512, "wdq%d" % a))
+            wdq.append(quantise(cast_weight([on_scalar, on_both][a], wd_raw[a], "wd_bf%d" % a), 512, "wdq%d" % a))
         wc8 = held("wc8", [P, 2 * N], U32)
         nc.vector.tensor_copy(
             wc8[:].rearrange("p (a i g m) -> p a g i m", a=2, i=4, m=4),
             wc8_raw[:].bitcast(U32).rearrange("p a (g m i) -> p a g i m", i=4, m=4),
         )
 
-        pages = [shared("page%d" % i, [P, T2], F32, "page%d" % i) for i in range(4)]
+        pages = [shared("page%d" % i, [P, T2], F32, tag) for i, tag in enumerate(["page0", "page1", "page2", "wd_bf1"])]
         for i in range(4):
             [nc.vector, nc.gpsimd][i // 2].memset(pages[i][:], 0.0)
 
@@ -198,17 +208,6 @@ def tile_list_profile_field_refresh_kernel(
 
         def stage2(s, i):
             j0, n = SLICES[s]
-            yd = ps2.tile([P, n], F32, name="yd", tag="y")
-            for a in range(2):
-                nc.tensor.matmul_mx(
-                    out=yd[:],
-                    lhsT=wdq[a][0][:, P * i : P * (i + 1)].bitcast(FP8X4),
-                    lhsT_scale=wdq[a][1][:, P * i : P * (i + 1)],
-                    rhs=hq[s, a][0][:].bitcast(FP8X4),
-                    rhs_scale=hq[s, a][1][:],
-                    start=(a == 0),
-                    stop=(a == 1),
-                )
             yc = ps2.tile([P, n], F32, name="yc", tag="y")
             for a in range(2):
                 col = N * a + P * i
@@ -221,27 +220,28 @@ def tile_list_profile_field_refresh_kernel(
                     start=(a == 0),
                     stop=(a == 1),
                 )
-            gate = ring.tile([P, n], F32, name="gate", tag="gate")
+            yd = ps2.tile([P, n], F32, name="yd", tag="y")
+            for a in range(2):
+                nc.tensor.matmul_mx(
+                    out=yd[:],
+                    lhsT=wdq[a][0][:, P * i : P * (i + 1)].bitcast(FP8X4),
+                    lhsT_scale=wdq[a][1][:, P * i : P * (i + 1)],
+                    rhs=hq[s, a][0][:].bitcast(FP8X4),
+                    rhs_scale=hq[s, a][1][:],
+                    start=(a == 0),
+                    stop=(a == 1),
+                )
+            gate = ring3.tile([P, n], F32, name="gate", tag="gate")
             nc.scalar.activation(gate[:], yd[:], ACT.Sigmoid, bias=bias[:, i : i + 1])
             y = ring3.tile([P, n], F32, name="y", tag="ysb")
             places = pages[i][:].indirect(scatter_list[:, j0 // 16 : (j0 + n) // 16])
-            if (s, i) == (0, 0):
-                nc.vector.tensor_tensor(y[:], yc[:], gate[:], ALU.mult)
-                nc.vector.tensor_tensor(places, y[:], wgo_sb[:, j0 : j0 + n], ALU.mult)
-            else:
-                yc_sb = ring.tile([P, n], F32, name="yc_sb", tag="yc_sb")
-                nc.scalar.copy(yc_sb[:], yc[:])
-                gw = ring.tile([P, n], F32, name="gw", tag="gw")
-                for c in range(0, n, 256):
-                    nc.gpsimd.tensor_tensor(gw[:, c : c + 256], gate[:, c : c + 256], wgo_sb[:, j0 + c : j0 + c + 256], ALU.mult)
-                    nc.gpsimd.tensor_tensor(y[:, c : c + 256], gw[:, c : c + 256], yc_sb[:, c : c + 256], ALU.mult)
-                nc.vector.tensor_copy(places, y[:])
+            nc.vector.tensor_tensor(y[:], yc[:], wgo_sb[:, j0 : j0 + n], ALU.mult)
+            nc.vector.tensor_tensor(places, y[:], gate[:], ALU.mult)
             if s == len(SLICES) - 1:
                 nc.sync.dma_start(out_rows[:, i, :], pages[i][:])
 
-        order = [(s, i) for s in range(2) for i in range(4)]
-        order = order + [(2, 0), (2, 1), (3, 0), (2, 2), (3, 1), (2, 3), (3, 2), (3, 3)]
-        halves = {0: (1, 0), 1: (1, 1), 3: (2, 0), 4: (2, 1), 6: (3, 0), 7: (3, 1)}
+        order = [(s, i) for s in range(3) for i in range(4)]
+        halves = {0: (1, 0), 1: (1, 1), 3: (2, 0), 5: (2, 1)}
         for step, (s, i) in enumerate(order):
             stage2(s, i)
             if step in halves:

@@ -46,53 +46,55 @@ def tile_list_profile_field_refresh_kernel(
             return keep.tile(shape, dtype, name=name, tag=tag, align_bytes=64)
 
         tab_s = held("tab_s", [P, T], U8)
-        w_s_raw = shared("w_s_raw", [P, H], U8, "w_s_raw")
-        planes = held("planes", [P, H + S], U8)
+        w_s_raw = held("w_s_raw", [P, 2 * H], U8)
+        planes = held("planes", [P, 2 * H + S], U8)
         nc.vector.memset(planes[:].bitcast(I32), 0)
         w_s = planes[:, 0:H]
-        v_s = planes[:, H : H + S]
+        wc8_s = planes[:, H : 2 * H]
+        v_s = planes[:, 2 * H : 2 * H + S]
+
+        def spread(rows):
+            return rows.bitcast(I32).unsqueeze(1).to_broadcast([16, 8, rows.shape[1] // 4])
 
         nc.sync.dma_start(gather_list[:], offs)
-        wb_rows = wb.rearrange("(p j) c -> p j c", j=4)
-        wb_raw = [shared("wb_raw%d" % b, [P, 4, 512], F32, "raw%d" % b) for b in range(2)]
-        nc.sync.dma_start(tab_s[:].bitcast(I32), tab_scales[0].bitcast(I32).unsqueeze(1).to_broadcast([16, 8, T // 4]))
-        nc.sync.dma_start(
-            w_s_raw[0:P:2, :].bitcast(I32), wa4_scales[0].bitcast(I32).unsqueeze(1).to_broadcast([16, 4, H // 4])
-        )
+        nc.sync.dma_start(tab_s[:].bitcast(I32), spread(tab_scales[0]))
+        nc.sync.dma_start(w_s_raw[:, 0:H].bitcast(I32), spread(wa4_scales[0]))
         for a in range(2):
-            nc.sync.dma_start(
-                w_s_raw[1:P:2, N * a : N * (a + 1)].bitcast(I32),
-                wc8_scales[a].bitcast(I32).unsqueeze(1).to_broadcast([16, 4, N // 4]),
-            )
+            nc.sync.dma_start(w_s_raw[:, H + N * a : H + N * (a + 1)].bitcast(I32), spread(wc8_scales[a]))
         bias = held("bias", [P, 4], F32)
         nc.sync.dma_start(bias[:], bd.rearrange("(p i) -> p i", i=4))
         nc.sync.dma_start(scatter_list[:], offs2)
+        wb_rows = wb.rearrange("(p j) c -> p j c", j=4)
+        wb_raw = [shared("wb_raw0", [P, 4, 512], F32, "raw0")]
         nc.sync.dma_start(wb_raw[0][:], wb_rows[:, :, 0:512])
-        wa4_raw = held("wa4_raw", [P, 2 * H], U8)
+        wa4_raw = shared("wa4_raw", [P, 2 * H], U8, "wa4_raw")
         nc.sync.dma_start(wa4_raw[:].bitcast(I32), wa4_words[0].bitcast(I32))
-        nc.sync.dma_start(wb_raw[1][:], wb_rows[:, :, 512:1024])
         tab_w = held("tab_w", [P, T], U32)
         nc.sync.dma_start(tab_w[:].bitcast(I32), tab_words[0].rearrange("p t i -> p (t i)").bitcast(I32))
+        wb_raw.append(shared("wb_raw1", [P, 4, 512], F32, "raw1"))
+        nc.sync.dma_start(wb_raw[1][:], wb_rows[:, :, 512:1024])
 
         v_s_g = held("v_s_g", [P, S], U8)
         nc.vector.tensor_copy(v_s_g[:], tab_s[:].indirect(gather_list[:]))
-        staged = held("staged", [P, H + S], U8)
-        nc.vector.tensor_copy(staged[:, H : H + S].bitcast(I32), v_s_g[:].bitcast(I32))
+        staged = shared("staged", [P, 2 * H + S], U8, "staged")
+        nc.vector.tensor_copy(staged[:, 2 * H : 2 * H + S].bitcast(I32), v_s_g[:].bitcast(I32))
         nc.vector.tensor_copy(
-            staged[:, 0:H].rearrange("p (b t m) -> p b t m", b=2, t=4),
-            w_s_raw[:].rearrange("p (b m t) -> p b t m", b=2, t=4),
+            staged[:, 0 : 2 * H].rearrange("p (b t m) -> p b t m", b=4, t=4),
+            w_s_raw[:].rearrange("p (b m t) -> p b t m", b=4, t=4),
         )
         for r in range(4):
             nc.sync.dma_start(planes[r:P:32, :].bitcast(I32), staged[8 * r : P : 32, :].bitcast(I32))
-
-        wd_raw = [shared("wd_raw0", [P, 4, N], F32, "w_s_raw")]
-        nc.sync.dma_start(wd_raw[0][:], wd[0:512, :].rearrange("(p j) c -> p j c", j=4))
 
         wa4 = held("wa4", [P, 2 * H], U8)
         nc.vector.tensor_copy(
             wa4[:].bitcast(U16).rearrange("p (b t m) -> p b t m", b=2, t=4),
             wa4_raw[:].bitcast(U16).rearrange("p (b m t) -> p b t m", b=2, t=4),
         )
+
+        v_w = []
+        for s, (j0, n) in enumerate(SLICES):
+            v_w.append(held("v_w%d" % s, [P, n], U32))
+            nc.vector.tensor_copy(v_w[s][:], tab_w[:].indirect(gather_list[:, j0 // 16 : (j0 + n) // 16]))
 
         def cast_weight(shares, raw, name):
             woven = shared(name, [P, 2048], BF16, name)
@@ -103,7 +105,7 @@ def tile_list_profile_field_refresh_kernel(
             return woven
 
         on_scalar = [(nc.scalar.copy, 0, P)]
-        on_both = [(nc.scalar.copy, 0, 64), (nc.vector.tensor_copy, 64, P)]
+        on_both = [(nc.vector.tensor_copy, 0, P)]
 
         def quantise(woven, width, name):
             codes = held(name + "_w", [P, width], U32)
@@ -111,84 +113,67 @@ def tile_list_profile_field_refresh_kernel(
             nc.vector.quantize_mx(out=codes[:].bitcast(FP8X4), scales=scales[:], in_=woven[:])
             return codes, scales
 
-        wbq = []
-        for b in range(2):
-            wbq.append(quantise(cast_weight(on_scalar, wb_raw[b], "wb_bf%d" % b), 512, "wbq%d" % b))
+        def load_wd(a, tag):
+            raw = shared("wd_raw%d" % a, [P, 4, N], F32, tag)
+            nc.sync.dma_start(raw[:], wd[512 * a : 512 * (a + 1), :].rearrange("(p j) c -> p j c", j=4))
+            return raw
 
-        wd_raw.append(shared("wd_raw1", [P, 4, N], F32, "raw0"))
-        nc.sync.dma_start(wd_raw[1][:], wd[512:1024, :].rearrange("(p j) c -> p j c", j=4))
-        wc8_raw = shared("wc8_raw", [P, 2, N], I32, "wb_bf0")
+        wb_bf0 = cast_weight(on_scalar, wb_raw[0], "wb_bf0")
+        wd_raw = [load_wd(0, "raw0")]
+        wbq = [quantise(wb_bf0, 512, "wbq0")]
+        wd_raw.append(load_wd(1, "staged"))
+        wb_bf1 = cast_weight(on_scalar, wb_raw[1], "wb_bf1")
+        wc8_raw = shared("wc8_raw", [P, 2, N], I32, "raw1")
         nc.sync.dma_start(wc8_raw[:], wc8_words.rearrange("a p c i -> p a (c i)").bitcast(I32))
-        wgo_sb = shared("wgo_sb", [P, S], F32, "raw1")
-        nc.sync.dma_start(wgo_sb[:], wgo)
-        wc8_s = shared("wc8_s", [P, H], U8, "wb_bf1")
-        nc.vector.memset(wc8_s[:].bitcast(I32), 0)
-        for r in range(4):
-            nc.sync.dma_start(wc8_s[r:P:32, :].bitcast(I32), staged[8 * r + 1 : P : 32, 0:H].bitcast(I32))
-
-        v_w = {}
-
-        def gather_words(s):
-            j0, n = SLICES[s]
-            v_w[s] = held("v_w%d" % s, [P, n], U32)
-            nc.vector.tensor_copy(v_w[s][:], tab_w[:].indirect(gather_list[:, j0 // 16 : (j0 + n) // 16]))
 
         def stage1(s, b):
             j0, n = SLICES[s]
-            if b == 0:
-                gather_words(s)
             h = ring.tile([P, 4 * n], BF16, name="h", tag="h", align_bytes=64)
             ha = ring.tile([P, 4 * n], F32 if s == 0 else BF16, name="ha", tag="ha", align_bytes=64)
             if s > 0:
                 hb = ring.tile([P, 4 * n], BF16, name="hb", tag="hb", align_bytes=64)
+
+            def product(c, weight, columns):
+                bank = ps1.tile([P, 4, P], F32, name="bank", tag="bank")
+                for t in range(4):
+                    codes, scales = columns(t)
+                    nc.tensor.matmul_mx(
+                        out=bank[:, t, :],
+                        lhsT=codes.bitcast(weight),
+                        lhsT_scale=scales,
+                        rhs=v_w[s][:, c * P : (c + 1) * P].bitcast(FP8X4),
+                        rhs_scale=v_s[:, j0 + c * P : j0 + (c + 1) * P],
+                        start=True,
+                        stop=True,
+                    )
+                return bank[:].rearrange("p t n -> p n t")
+
+            def wa4_columns(t):
+                col = 512 * b + P * t
+                return wa4[:, 2 * col : 2 * (col + P)], w_s[:, col : col + P]
+
+            def wb_columns(t):
+                return wbq[b][0][:, P * t : P * (t + 1)], wbq[b][1][:, P * t : P * (t + 1)]
+
+            def part(tile, c):
+                return tile[:, 512 * c : 512 * (c + 1)].rearrange("p (n t) -> p n t", t=4)
+
             for c in range(n // P):
-                rhs = v_w[s][:, c * P : (c + 1) * P].bitcast(FP8X4)
-                rhs_scale = v_s[:, j0 + c * P : j0 + (c + 1) * P]
-                bank_a = ps1.tile([P, 4, P], F32, name="bank_a", tag="bank")
-                for t in range(4):
-                    col = 512 * b + P * t
-                    nc.tensor.matmul_mx(
-                        out=bank_a[:, t, :],
-                        lhsT=wa4[:, 2 * col : 2 * (col + P)].bitcast(FP4X4),
-                        lhsT_scale=w_s[:, col : col + P],
-                        rhs=rhs,
-                        rhs_scale=rhs_scale,
-                        start=True,
-                        stop=True,
-                    )
-                nc.scalar.copy(
-                    ha[:, 512 * c : 512 * (c + 1)].rearrange("p (n t) -> p n t", t=4),
-                    bank_a[:].rearrange("p t n -> p n t"),
-                )
-                bank_b = ps1.tile([P, 4, P], F32, name="bank_b", tag="bank")
-                for t in range(4):
-                    nc.tensor.matmul_mx(
-                        out=bank_b[:, t, :],
-                        lhsT=wbq[b][0][:, P * t : P * (t + 1)].bitcast(FP8X4),
-                        lhsT_scale=wbq[b][1][:, P * t : P * (t + 1)],
-                        rhs=rhs,
-                        rhs_scale=rhs_scale,
-                        start=True,
-                        stop=True,
-                    )
+                nc.scalar.copy(part(ha, c), product(c, FP4X4, wa4_columns))
+            for c in range(n // P):
                 if s == 0:
-                    nc.vector.tensor_tensor(
-                        h[:, 512 * c : 512 * (c + 1)].rearrange("p (n t) -> p n t", t=4),
-                        bank_b[:].rearrange("p t n -> p n t"),
-                        ha[:, 512 * c : 512 * (c + 1)].rearrange("p (n t) -> p n t", t=4),
-                        ALU.max,
-                    )
+                    nc.vector.tensor_tensor(part(h, c), product(c, FP8X4, wb_columns), part(ha, c), ALU.max)
                 else:
-                    nc.scalar.copy(
-                        hb[:, 512 * c : 512 * (c + 1)].rearrange("p (n t) -> p n t", t=4),
-                        bank_b[:].rearrange("p t n -> p n t"),
-                    )
+                    nc.scalar.copy(part(hb, c), product(c, FP8X4, wb_columns))
             if s > 0:
                 nc.vector.tensor_tensor(h[:], ha[:], hb[:], ALU.max)
             hq[s, b] = quantise(h, n, "hq%d_%d" % (s, b))
 
         hq = {}
         stage1(0, 0)
+        wbq.append(quantise(wb_bf1, 512, "wbq1"))
+        wgo_sb = shared("wgo_sb", [P, S], F32, "wb_bf1")
+        nc.sync.dma_start(wgo_sb[:], wgo)
         stage1(0, 1)
 
         wdq = []
@@ -200,13 +185,13 @@ def tile_list_profile_field_refresh_kernel(
             wc8_raw[:].bitcast(U32).rearrange("p a (g m i) -> p a g i m", i=4, m=4),
         )
 
-        pages = [shared("page%d" % i, [P, T2], F32, tag) for i, tag in enumerate(["page0", "page1", "page2", "wd_bf1"])]
+        pages = [shared("page%d" % i, [P, T2], F32, tag) for i, tag in enumerate(["page0", "page2", "wb_bf0", "wd_bf1"])]
         for i in range(4):
-            [nc.vector, nc.gpsimd][i // 2].memset(pages[i][:], 0.0)
+            [nc.vector, nc.gpsimd][min(i, 1)].memset(pages[i][:], 0.0)
 
         out_rows = out.rearrange("(p i) t -> p i t", i=4)
 
-        def stage2(s, i):
+        def stage2(s, i, step):
             j0, n = SLICES[s]
             yc = ps2.tile([P, n], F32, name="yc", tag="y")
             for a in range(2):
@@ -231,18 +216,43 @@ def tile_list_profile_field_refresh_kernel(
                     start=(a == 0),
                     stop=(a == 1),
                 )
-            gate = ring3.tile([P, n], F32, name="gate", tag="gate")
+            weights = wgo_sb[:, j0 : j0 + n]
+            if step == 5:
+                gate = ring.tile([P, n], F32, name="gate", tag="half")
+            else:
+                gate = ring3.tile([P, n], F32, name="gate", tag="gate")
             nc.scalar.activation(gate[:], yd[:], ACT.Sigmoid, bias=bias[:, i : i + 1])
+
             y = ring3.tile([P, n], F32, name="y", tag="ysb")
+            if step < 5:
+                nc.vector.tensor_tensor(y[:], yc[:], weights, ALU.mult)
+                return y, gate
+            half = ring.tile([P, n], F32, name="half", tag="half")
+            if step < 8:
+                nc.vector.tensor_tensor(half[:], yc[:], weights, ALU.mult)
+            else:
+                yc_sb = ring.tile([P, n], F32, name="yc_sb", tag="yc_sb")
+                nc.scalar.copy(yc_sb[:], yc[:])
+                nc.gpsimd.tensor_tensor(half[:], yc_sb[:], weights, ALU.mult)
+            [nc.gpsimd, nc.vector][step == 5].tensor_tensor(y[:], half[:], gate[:], ALU.mult)
+            return y, None
+
+        def scatter(s, i, y, gate):
+            j0, n = SLICES[s]
             places = pages[i][:].indirect(scatter_list[:, j0 // 16 : (j0 + n) // 16])
-            nc.vector.tensor_tensor(y[:], yc[:], wgo_sb[:, j0 : j0 + n], ALU.mult)
-            nc.vector.tensor_tensor(places, y[:], gate[:], ALU.mult)
+            if gate is None:
+                nc.vector.tensor_copy(places, y[:])
+            else:
+                nc.vector.tensor_tensor(places, y[:], gate[:], ALU.mult)
             if s == len(SLICES) - 1:
                 nc.sync.dma_start(out_rows[:, i, :], pages[i][:])
 
         order = [(s, i) for s in range(3) for i in range(4)]
-        halves = {0: (1, 0), 1: (1, 1), 3: (2, 0), 5: (2, 1)}
+        halves = {0: (1, 0), 1: (1, 1), 2: (2, 0), 4: (2, 1)}
+        made = [stage2(0, 0, 0)]
         for step, (s, i) in enumerate(order):
-            stage2(s, i)
             if step in halves:
                 stage1(*halves[step])
+            if step + 1 < len(order):
+                made.append(stage2(*order[step + 1], step + 1))
+            scatter(s, i, *made[step])

@@ -37,20 +37,25 @@ def tile_list_profile_field_refresh_kernel(
         gather_list = keep.tile([P, S // 16], U16, name="gather_list")
         scatter_list = keep.tile([P, S // 16], U16, name="scatter_list")
 
-        warm = keep.tile([P, 8], F32, name="warm", tag="page2", align_bytes=64)
-        warm_out = keep.tile([P, 8], F32, name="warm_out", align_bytes=64)
-        nc.vector.memset(warm[:], 0.0)
-        nc.scalar.activation(warm_out[:], warm[:], ACT.Sigmoid)
-
         def shared(name, shape, dtype, tag):
             return keep.tile(shape, dtype, name=name, tag=tag, align_bytes=64)
 
+        warm = held("warm", [P, 1], F32)
+        warm_out = held("warm_out", [P, 1], F32)
+        nc.vector.memset(warm[:], 0.0)
+        nc.scalar.activation(warm_out[:], warm[:], ACT.Sigmoid)
+
         tab_s = held("tab_s", [P, T], U8)
-        w_s_raw = held("w_s_raw", [P, 2 * H], U8)
+        wa4_s_raw = shared("wa4_s_raw", [P, H], U8, "wa4_s_raw")
+        staged = shared("staged", [P, 2 * H + S], U8, "staged")
         planes = held("planes", [P, 2 * H + S], U8)
-        nc.vector.memset(planes[:].bitcast(I32), 0)
+        pages = [held("page%d" % i, [P, T2], F32) for i in range(3)]
+        nc.gpsimd.memset(pages[0][:], 0.0)
+        nc.gpsimd.memset(pages[1][:], 0.0)
+        nc.gpsimd.memset(planes[:].bitcast(I32), 0)
+        nc.vector.memset(pages[2][:, 0 : T2 // 2 - 1], 0.0)
+        nc.vector.memset(pages[2][:, T2 // 2 - 1 : T2], 0.0)
         w_s = planes[:, 0:H]
-        wc8_s = planes[:, H : 2 * H]
         v_s = planes[:, 2 * H : 2 * H + S]
 
         def spread(rows):
@@ -58,32 +63,42 @@ def tile_list_profile_field_refresh_kernel(
 
         nc.sync.dma_start(gather_list[:], offs)
         nc.sync.dma_start(tab_s[:].bitcast(I32), spread(tab_scales[0]))
-        nc.sync.dma_start(w_s_raw[:, 0:H].bitcast(I32), spread(wa4_scales[0]))
+        nc.sync.dma_start(wa4_s_raw[:].bitcast(I32), spread(wa4_scales[0]))
         for a in range(2):
-            nc.sync.dma_start(w_s_raw[:, H + N * a : H + N * (a + 1)].bitcast(I32), spread(wc8_scales[a]))
-        bias = held("bias", [P, 4], F32)
-        nc.sync.dma_start(bias[:], bd.rearrange("(p i) -> p i", i=4))
-        nc.sync.dma_start(scatter_list[:], offs2)
+            nc.sync.dma_start(staged[:, H + N * a : H + N * (a + 1)].bitcast(I32), spread(wc8_scales[a]))
+        tab_w = held("tab_w", [P, T], U32)
+        nc.sync.dma_start(tab_w[:].bitcast(I32), tab_words[0].rearrange("p t i -> p (t i)").bitcast(I32))
         wb_rows = wb.rearrange("(p j) c -> p j c", j=4)
         wb_raw = [shared("wb_raw0", [P, 4, 512], F32, "raw0")]
         nc.sync.dma_start(wb_raw[0][:], wb_rows[:, :, 0:512])
-        wa4_raw = shared("wa4_raw", [P, 2 * H], U8, "wa4_raw")
+        wa4_raw = held("wa4_raw", [P, 2 * H], U8)
         nc.sync.dma_start(wa4_raw[:].bitcast(I32), wa4_words[0].bitcast(I32))
-        tab_w = held("tab_w", [P, T], U32)
-        nc.sync.dma_start(tab_w[:].bitcast(I32), tab_words[0].rearrange("p t i -> p (t i)").bitcast(I32))
-        wb_raw.append(shared("wb_raw1", [P, 4, 512], F32, "raw1"))
+        wb_raw.append(held("wb_raw1", [P, 4, 512], F32))
         nc.sync.dma_start(wb_raw[1][:], wb_rows[:, :, 512:1024])
+        nc.sync.dma_start(scatter_list[:], offs2)
 
-        v_s_g = held("v_s_g", [P, S], U8)
+        v_s_g = shared("v_s_g", [P, S], U8, "v_s_g")
         nc.vector.tensor_copy(v_s_g[:], tab_s[:].indirect(gather_list[:]))
-        staged = shared("staged", [P, 2 * H + S], U8, "staged")
         nc.vector.tensor_copy(staged[:, 2 * H : 2 * H + S].bitcast(I32), v_s_g[:].bitcast(I32))
         nc.vector.tensor_copy(
-            staged[:, 0 : 2 * H].rearrange("p (b t m) -> p b t m", b=4, t=4),
-            w_s_raw[:].rearrange("p (b m t) -> p b t m", b=4, t=4),
+            staged[:, 0:H].rearrange("p (b t m) -> p b t m", b=2, t=4),
+            wa4_s_raw[:].rearrange("p (b m t) -> p b t m", b=2, t=4),
         )
         for r in range(4):
-            nc.sync.dma_start(planes[r:P:32, :].bitcast(I32), staged[8 * r : P : 32, :].bitcast(I32))
+            nc.scalar.dma_start(planes[r:P:32, :].bitcast(I32), staged[8 * r : P : 32, :].bitcast(I32))
+        pages.append(shared("page3", [P, T2], F32, "v_s_g"))
+        nc.gpsimd.memset(pages[3][:], 0.0)
+
+        wd_raw = shared("wd_raw", [P, 2, 4, N], F32, "wa4_s_raw")
+        for a in range(2):
+            nc.sync.dma_start(wd_raw[:, a], wd[512 * a : 512 * (a + 1), :].rearrange("(p j) c -> p j c", j=4))
+        wc8_raw = shared("wc8_raw", [P, 2, N], I32, "staged")
+        nc.sync.dma_start(wc8_raw[:], wc8_words.rearrange("a p c i -> p a (c i)").bitcast(I32))
+
+        v_w = []
+        for s, (j0, n) in enumerate(SLICES):
+            v_w.append(held("v_w%d" % s, [P, n], U32))
+            nc.vector.tensor_copy(v_w[s][:], tab_w[:].indirect(gather_list[:, j0 // 16 : (j0 + n) // 16]))
 
         wa4 = held("wa4", [P, 2 * H], U8)
         nc.vector.tensor_copy(
@@ -91,21 +106,17 @@ def tile_list_profile_field_refresh_kernel(
             wa4_raw[:].bitcast(U16).rearrange("p (b m t) -> p b t m", b=2, t=4),
         )
 
-        v_w = []
-        for s, (j0, n) in enumerate(SLICES):
-            v_w.append(held("v_w%d" % s, [P, n], U32))
-            nc.vector.tensor_copy(v_w[s][:], tab_w[:].indirect(gather_list[:, j0 // 16 : (j0 + n) // 16]))
-
         def cast_weight(shares, raw, name):
-            woven = shared(name, [P, 2048], BF16, name)
+            woven = held(name, [P, 2048], BF16)
             dst = woven[:].rearrange("p (t m j) -> p m t j", t=4, j=4)
-            src = raw[:].rearrange("p j (m t) -> p m t j", t=4)
+            src = raw.rearrange("p j (m t) -> p m t j", t=4)
             for copy, m0, m1 in shares:
                 copy(dst[:, m0:m1], src[:, m0:m1])
             return woven
 
         on_scalar = [(nc.scalar.copy, 0, P)]
-        on_both = [(nc.vector.tensor_copy, 0, P)]
+        on_vector = [(nc.vector.tensor_copy, 0, P)]
+        on_both = [(nc.scalar.copy, 0, P // 2), (nc.vector.tensor_copy, P // 2, P)]
 
         def quantise(woven, width, name):
             codes = held(name + "_w", [P, width], U32)
@@ -113,25 +124,19 @@ def tile_list_profile_field_refresh_kernel(
             nc.vector.quantize_mx(out=codes[:].bitcast(FP8X4), scales=scales[:], in_=woven[:])
             return codes, scales
 
-        def load_wd(a, tag):
-            raw = shared("wd_raw%d" % a, [P, 4, N], F32, tag)
-            nc.sync.dma_start(raw[:], wd[512 * a : 512 * (a + 1), :].rearrange("(p j) c -> p j c", j=4))
-            return raw
-
-        wb_bf0 = cast_weight(on_scalar, wb_raw[0], "wb_bf0")
-        wd_raw = [load_wd(0, "raw0")]
-        wbq = [quantise(wb_bf0, 512, "wbq0")]
-        wd_raw.append(load_wd(1, "staged"))
-        wb_bf1 = cast_weight(on_scalar, wb_raw[1], "wb_bf1")
-        wc8_raw = shared("wc8_raw", [P, 2, N], I32, "raw1")
-        nc.sync.dma_start(wc8_raw[:], wc8_words.rearrange("a p c i -> p a (c i)").bitcast(I32))
+        wbq = [quantise(cast_weight(on_scalar, wb_raw[0][:], "wb_bf0"), 512, "wbq0")]
+        late = shared("late", [P, S + 8], F32, "raw0")
+        wgo_sb = late[:, 0:S]
+        bias = late[:, S : S + 4]
+        nc.sync.dma_start(wgo_sb, wgo)
+        nc.sync.dma_start(bias, bd.rearrange("(p i) -> p i", i=4))
+        wbq.append(quantise(cast_weight(on_vector, wb_raw[1][:], "wb_bf1"), 512, "wbq1"))
 
         def stage1(s, b):
             j0, n = SLICES[s]
             h = ring.tile([P, 4 * n], BF16, name="h", tag="h", align_bytes=64)
-            ha = ring.tile([P, 4 * n], F32 if s == 0 else BF16, name="ha", tag="ha", align_bytes=64)
-            if s > 0:
-                hb = ring.tile([P, 4 * n], BF16, name="hb", tag="hb", align_bytes=64)
+            ha = ring.tile([P, 4 * n], BF16, name="ha", tag="ha", align_bytes=64)
+            hb = ring.tile([P, 4 * n], BF16, name="hb", tag="hb", align_bytes=64)
 
             def product(c, weight, columns):
                 bank = ps1.tile([P, 4, P], F32, name="bank", tag="bank")
@@ -161,33 +166,25 @@ def tile_list_profile_field_refresh_kernel(
             for c in range(n // P):
                 nc.scalar.copy(part(ha, c), product(c, FP4X4, wa4_columns))
             for c in range(n // P):
-                if s == 0:
-                    nc.vector.tensor_tensor(part(h, c), product(c, FP8X4, wb_columns), part(ha, c), ALU.max)
-                else:
-                    nc.scalar.copy(part(hb, c), product(c, FP8X4, wb_columns))
-            if s > 0:
-                nc.vector.tensor_tensor(h[:], ha[:], hb[:], ALU.max)
+                nc.scalar.copy(part(hb, c), product(c, FP8X4, wb_columns))
+            nc.vector.tensor_tensor(h[:], ha[:], hb[:], ALU.max)
             hq[s, b] = quantise(h, n, "hq%d_%d" % (s, b))
 
         hq = {}
         stage1(0, 0)
-        wbq.append(quantise(wb_bf1, 512, "wbq1"))
-        wgo_sb = shared("wgo_sb", [P, S], F32, "wb_bf1")
-        nc.sync.dma_start(wgo_sb[:], wgo)
+        wdq = [quantise(cast_weight(on_vector, wd_raw[:, 0], "wd_bf0"), 512, "wdq0")]
         stage1(0, 1)
-
-        wdq = []
-        for a in range(2):
-            wdq.append(quantise(cast_weight([on_scalar, on_both][a], wd_raw[a], "wd_bf%d" % a), 512, "wdq%d" % a))
+        wdq.append(quantise(cast_weight(on_both, wd_raw[:, 1], "wd_bf1"), 512, "wdq1"))
+        wc8_s = held("wc8_s", [P, H], U8)
+        nc.vector.tensor_copy(
+            wc8_s[:].rearrange("p (b t m) -> p b t m", b=2, t=4),
+            planes[:, H : 2 * H].rearrange("p (b m t) -> p b t m", b=2, t=4),
+        )
         wc8 = held("wc8", [P, 2 * N], U32)
         nc.vector.tensor_copy(
             wc8[:].rearrange("p (a i g m) -> p a g i m", a=2, i=4, m=4),
             wc8_raw[:].bitcast(U32).rearrange("p a (g m i) -> p a g i m", i=4, m=4),
         )
-
-        pages = [shared("page%d" % i, [P, T2], F32, tag) for i, tag in enumerate(["page0", "page2", "wb_bf0", "wd_bf1"])]
-        for i in range(4):
-            [nc.vector, nc.gpsimd][min(i, 1)].memset(pages[i][:], 0.0)
 
         out_rows = out.rearrange("(p i) t -> p i t", i=4)
 

@@ -47,6 +47,7 @@ def tile_list_profile_field_refresh_kernel(
 
         tab_s = held("tab_s", [P, T], U8)
         wa4_s_raw = shared("wa4_s_raw", [P, H], U8, "wa4_s_raw")
+        wc8_s_raw = held("wc8_s_raw", [P, H], U8)
         staged = shared("staged", [P, 2 * H + S], U8, "staged")
         planes = held("planes", [P, 2 * H + S], U8)
         pages = [held("page%d" % i, [P, T2], F32) for i in range(3)]
@@ -56,6 +57,7 @@ def tile_list_profile_field_refresh_kernel(
         nc.vector.memset(pages[2][:, 0 : T2 // 2 - 1], 0.0)
         nc.vector.memset(pages[2][:, T2 // 2 - 1 : T2], 0.0)
         w_s = planes[:, 0:H]
+        wc8_s = planes[:, H : 2 * H]
         v_s = planes[:, 2 * H : 2 * H + S]
 
         def spread(rows):
@@ -65,40 +67,34 @@ def tile_list_profile_field_refresh_kernel(
         nc.sync.dma_start(tab_s[:].bitcast(I32), spread(tab_scales[0]))
         nc.sync.dma_start(wa4_s_raw[:].bitcast(I32), spread(wa4_scales[0]))
         for a in range(2):
-            nc.sync.dma_start(staged[:, H + N * a : H + N * (a + 1)].bitcast(I32), spread(wc8_scales[a]))
-        tab_w = held("tab_w", [P, T], U32)
-        nc.sync.dma_start(tab_w[:].bitcast(I32), tab_words[0].rearrange("p t i -> p (t i)").bitcast(I32))
+            nc.sync.dma_start(wc8_s_raw[:, N * a : N * (a + 1)].bitcast(I32), spread(wc8_scales[a]))
         wb_rows = wb.rearrange("(p j) c -> p j c", j=4)
         wb_raw = [shared("wb_raw0", [P, 4, 512], F32, "raw0")]
         nc.sync.dma_start(wb_raw[0][:], wb_rows[:, :, 0:512])
         wa4_raw = held("wa4_raw", [P, 2 * H], U8)
         nc.sync.dma_start(wa4_raw[:].bitcast(I32), wa4_words[0].bitcast(I32))
-        wb_raw.append(held("wb_raw1", [P, 4, 512], F32))
-        nc.sync.dma_start(wb_raw[1][:], wb_rows[:, :, 512:1024])
+        tab_w = held("tab_w", [P, T], U32)
+        nc.sync.dma_start(tab_w[:].bitcast(I32), tab_words[0].rearrange("p t i -> p (t i)").bitcast(I32))
         nc.sync.dma_start(scatter_list[:], offs2)
 
         v_s_g = shared("v_s_g", [P, S], U8, "v_s_g")
         nc.vector.tensor_copy(v_s_g[:], tab_s[:].indirect(gather_list[:]))
         nc.vector.tensor_copy(staged[:, 2 * H : 2 * H + S].bitcast(I32), v_s_g[:].bitcast(I32))
-        nc.vector.tensor_copy(
-            staged[:, 0:H].rearrange("p (b t m) -> p b t m", b=2, t=4),
-            wa4_s_raw[:].rearrange("p (b m t) -> p b t m", b=2, t=4),
-        )
+        for raw, c0 in ((wc8_s_raw, H), (wa4_s_raw, 0)):
+            nc.vector.tensor_copy(
+                staged[:, c0 : c0 + H].rearrange("p (b t m) -> p b t m", b=2, t=4),
+                raw[:].rearrange("p (b m t) -> p b t m", b=2, t=4),
+            )
         for r in range(4):
-            nc.scalar.dma_start(planes[r:P:32, :].bitcast(I32), staged[8 * r : P : 32, :].bitcast(I32))
-        pages.append(shared("page3", [P, T2], F32, "v_s_g"))
-        nc.gpsimd.memset(pages[3][:], 0.0)
+            nc.sync.dma_start(planes[r:P:32, :].bitcast(I32), staged[8 * r : P : 32, :].bitcast(I32))
 
-        wd_raw = shared("wd_raw", [P, 2, 4, N], F32, "wa4_s_raw")
+        w_raw = shared("w_raw", [P, 3, 4, N], F32, "wa4_s_raw")
+        nc.sync.dma_start(w_raw[:, 2], wb_rows[:, :, 512:1024])
+        wd_raw = w_raw[:, 0:2]
         for a in range(2):
             nc.sync.dma_start(wd_raw[:, a], wd[512 * a : 512 * (a + 1), :].rearrange("(p j) c -> p j c", j=4))
         wc8_raw = shared("wc8_raw", [P, 2, N], I32, "staged")
         nc.sync.dma_start(wc8_raw[:], wc8_words.rearrange("a p c i -> p a (c i)").bitcast(I32))
-
-        v_w = []
-        for s, (j0, n) in enumerate(SLICES):
-            v_w.append(held("v_w%d" % s, [P, n], U32))
-            nc.vector.tensor_copy(v_w[s][:], tab_w[:].indirect(gather_list[:, j0 // 16 : (j0 + n) // 16]))
 
         wa4 = held("wa4", [P, 2 * H], U8)
         nc.vector.tensor_copy(
@@ -107,14 +103,14 @@ def tile_list_profile_field_refresh_kernel(
         )
 
         def cast_weight(shares, raw, name):
-            woven = held(name, [P, 2048], BF16)
-            dst = woven[:].rearrange("p (t m j) -> p m t j", t=4, j=4)
-            src = raw.rearrange("p j (m t) -> p m t j", t=4)
+            woven = shared(name, [P, 2048], BF16, name)
+            dst = woven[:].rearrange("p (t m j) -> p m j t", t=4, j=4)
+            src = raw.rearrange("p j (m t) -> p m j t", t=4)
             for copy, m0, m1 in shares:
                 copy(dst[:, m0:m1], src[:, m0:m1])
             return woven
 
-        on_scalar = [(nc.scalar.copy, 0, P)]
+        mostly_scalar = [(nc.scalar.copy, 0, 96), (nc.vector.tensor_copy, 96, P)]
         on_vector = [(nc.vector.tensor_copy, 0, P)]
         on_both = [(nc.scalar.copy, 0, P // 2), (nc.vector.tensor_copy, P // 2, P)]
 
@@ -124,13 +120,20 @@ def tile_list_profile_field_refresh_kernel(
             nc.vector.quantize_mx(out=codes[:].bitcast(FP8X4), scales=scales[:], in_=woven[:])
             return codes, scales
 
-        wbq = [quantise(cast_weight(on_scalar, wb_raw[0][:], "wb_bf0"), 512, "wbq0")]
+        wbq = [quantise(cast_weight(mostly_scalar, wb_raw[0][:], "wb_bf0"), 512, "wbq0")]
+        pages.append(shared("page3", [P, T2], F32, "wb_bf0"))
+        nc.gpsimd.memset(pages[3][:], 0.0)
+        v_w = []
+        for s, (j0, n) in enumerate(SLICES):
+            v_w.append(held("v_w%d" % s, [P, n], U32))
+            nc.vector.tensor_copy(v_w[s][:], tab_w[:].indirect(gather_list[:, j0 // 16 : (j0 + n) // 16]))
+
         late = shared("late", [P, S + 8], F32, "raw0")
         wgo_sb = late[:, 0:S]
         bias = late[:, S : S + 4]
         nc.sync.dma_start(wgo_sb, wgo)
         nc.sync.dma_start(bias, bd.rearrange("(p i) -> p i", i=4))
-        wbq.append(quantise(cast_weight(on_vector, wb_raw[1][:], "wb_bf1"), 512, "wbq1"))
+        wbq.append(quantise(cast_weight(on_vector, w_raw[:, 2], "wb_bf1"), 512, "wbq1"))
 
         def stage1(s, b):
             j0, n = SLICES[s]
@@ -174,12 +177,8 @@ def tile_list_profile_field_refresh_kernel(
         stage1(0, 0)
         wdq = [quantise(cast_weight(on_vector, wd_raw[:, 0], "wd_bf0"), 512, "wdq0")]
         stage1(0, 1)
+        stage1(1, 0)
         wdq.append(quantise(cast_weight(on_both, wd_raw[:, 1], "wd_bf1"), 512, "wdq1"))
-        wc8_s = held("wc8_s", [P, H], U8)
-        nc.vector.tensor_copy(
-            wc8_s[:].rearrange("p (b t m) -> p b t m", b=2, t=4),
-            planes[:, H : 2 * H].rearrange("p (b m t) -> p b t m", b=2, t=4),
-        )
         wc8 = held("wc8", [P, 2 * N], U32)
         nc.vector.tensor_copy(
             wc8[:].rearrange("p (a i g m) -> p a g i m", a=2, i=4, m=4),
@@ -245,7 +244,7 @@ def tile_list_profile_field_refresh_kernel(
                 nc.sync.dma_start(out_rows[:, i, :], pages[i][:])
 
         order = [(s, i) for s in range(3) for i in range(4)]
-        halves = {0: (1, 0), 1: (1, 1), 2: (2, 0), 4: (2, 1)}
+        halves = {0: (1, 1), 1: (2, 0), 3: (2, 1)}
         made = [stage2(0, 0, 0)]
         for step, (s, i) in enumerate(order):
             if step in halves:

@@ -50,12 +50,12 @@ def tile_list_profile_field_refresh_kernel(
         wc8_s_raw = held("wc8_s_raw", [P, H], U8)
         staged = shared("staged", [P, 2 * H + S], U8, "staged")
         planes = held("planes", [P, 2 * H + S], U8)
-        pages = [held("page%d" % i, [P, T2], F32) for i in range(3)]
-        nc.gpsimd.memset(pages[0][:], 0.0)
-        nc.gpsimd.memset(pages[1][:], 0.0)
+        pages = {i: held("page%d" % i, [P, T2], F32) for i in (0, 2)}
         nc.gpsimd.memset(planes[:].bitcast(I32), 0)
-        nc.vector.memset(pages[2][:, 0 : T2 // 2 - 1], 0.0)
-        nc.vector.memset(pages[2][:, T2 // 2 - 1 : T2], 0.0)
+        nc.gpsimd.memset(pages[0][:], 0.0)
+        nc.gpsimd.memset(pages[2][:, T2 // 2 : T2], 0.0)
+        nc.vector.memset(pages[2][:, 0 : T2 // 4 - 1], 0.0)
+        nc.vector.memset(pages[2][:, T2 // 4 - 1 : T2 // 2], 0.0)
         w_s = planes[:, 0:H]
         wc8_s = planes[:, H : 2 * H]
         v_s = planes[:, 2 * H : 2 * H + S]
@@ -121,8 +121,8 @@ def tile_list_profile_field_refresh_kernel(
             return codes, scales
 
         wbq = [quantise(cast_weight(mostly_scalar, wb_raw[0][:], "wb_bf0"), 512, "wbq0")]
-        pages.append(shared("page3", [P, T2], F32, "wb_bf0"))
-        nc.gpsimd.memset(pages[3][:], 0.0)
+        pages[1] = shared("page1", [P, T2], F32, "wb_bf0")
+        nc.gpsimd.memset(pages[1][:], 0.0)
         v_w = []
         for s, (j0, n) in enumerate(SLICES):
             v_w.append(held("v_w%d" % s, [P, n], U32))
@@ -137,7 +137,10 @@ def tile_list_profile_field_refresh_kernel(
 
         def stage1(s, b):
             j0, n = SLICES[s]
-            h = ring.tile([P, 4 * n], BF16, name="h", tag="h", align_bytes=64)
+            if (s, b) == (1, 1):
+                h = shared("h11", [P, 4 * n], BF16, "h11")
+            else:
+                h = ring.tile([P, 4 * n], BF16, name="h", tag="h", align_bytes=64)
             ha = ring.tile([P, 4 * n], BF16, name="ha", tag="ha", align_bytes=64)
             hb = ring.tile([P, 4 * n], BF16, name="hb", tag="hb", align_bytes=64)
 
@@ -181,8 +184,8 @@ def tile_list_profile_field_refresh_kernel(
         wdq.append(quantise(cast_weight(on_both, wd_raw[:, 1], "wd_bf1"), 512, "wdq1"))
         wc8 = held("wc8", [P, 2 * N], U32)
         nc.vector.tensor_copy(
-            wc8[:].rearrange("p (a i g m) -> p a g i m", a=2, i=4, m=4),
-            wc8_raw[:].bitcast(U32).rearrange("p a (g m i) -> p a g i m", i=4, m=4),
+            wc8[:].rearrange("p (a i g m) -> p a g m i", a=2, i=4, m=4),
+            wc8_raw[:].bitcast(U32).rearrange("p a (g m i) -> p a g m i", i=4, m=4),
         )
 
         out_rows = out.rearrange("(p i) t -> p i t", i=4)
@@ -249,6 +252,9 @@ def tile_list_profile_field_refresh_kernel(
         for step, (s, i) in enumerate(order):
             if step in halves:
                 stage1(*halves[step])
+            if step == 0:
+                pages[3] = shared("page3", [P, T2], F32, "h11")
+                nc.gpsimd.memset(pages[3][:], 0.0)
             if step + 1 < len(order):
                 made.append(stage2(*order[step + 1], step + 1))
             scatter(s, i, *made[step])

@@ -47,17 +47,15 @@ def tile_list_profile_field_refresh_kernel(
 
         tab_s = held("tab_s", [P, T], U8)
         wa4_s_raw = shared("wa4_s_raw", [P, H], U8, "wa4_s_raw")
-        wc8_s_raw = held("wc8_s_raw", [P, H], U8)
         staged = shared("staged", [P, 2 * H + S], U8, "staged")
         planes = held("planes", [P, 2 * H + S], U8)
-        pages = {i: held("page%d" % i, [P, T2], F32) for i in (0, 2)}
+        pages = [held("page%d" % i, [P, T2], F32) for i in range(3)]
         nc.gpsimd.memset(planes[:].bitcast(I32), 0)
         nc.gpsimd.memset(pages[0][:], 0.0)
-        nc.gpsimd.memset(pages[2][:, T2 // 2 : T2], 0.0)
-        nc.vector.memset(pages[2][:, 0 : T2 // 4 - 1], 0.0)
-        nc.vector.memset(pages[2][:, T2 // 4 - 1 : T2 // 2], 0.0)
+        nc.gpsimd.memset(pages[1][:], 0.0)
+        nc.vector.memset(pages[2][:, 0 : T2 // 2 - 1], 0.0)
+        nc.vector.memset(pages[2][:, T2 // 2 - 1 : T2], 0.0)
         w_s = planes[:, 0:H]
-        wc8_s = planes[:, H : 2 * H]
         v_s = planes[:, 2 * H : 2 * H + S]
 
         def spread(rows):
@@ -67,34 +65,28 @@ def tile_list_profile_field_refresh_kernel(
         nc.sync.dma_start(tab_s[:].bitcast(I32), spread(tab_scales[0]))
         nc.sync.dma_start(wa4_s_raw[:].bitcast(I32), spread(wa4_scales[0]))
         for a in range(2):
-            nc.sync.dma_start(wc8_s_raw[:, N * a : N * (a + 1)].bitcast(I32), spread(wc8_scales[a]))
+            nc.sync.dma_start(staged[:, H + N * a : H + N * (a + 1)].bitcast(I32), spread(wc8_scales[a]))
         wb_rows = wb.rearrange("(p j) c -> p j c", j=4)
         wb_raw = [shared("wb_raw0", [P, 4, 512], F32, "raw0")]
         nc.sync.dma_start(wb_raw[0][:], wb_rows[:, :, 0:512])
-        wa4_raw = held("wa4_raw", [P, 2 * H], U8)
-        nc.sync.dma_start(wa4_raw[:].bitcast(I32), wa4_words[0].bitcast(I32))
-        tab_w = held("tab_w", [P, T], U32)
+        tab_w = shared("tab_w", [P, T], U32, "tab_w")
         nc.sync.dma_start(tab_w[:].bitcast(I32), tab_words[0].rearrange("p t i -> p (t i)").bitcast(I32))
+        wa4_raw = shared("wa4_raw", [P, 2 * H], U8, "wa4_raw")
+        nc.sync.dma_start(wa4_raw[:].bitcast(I32), wa4_words[0].bitcast(I32))
         nc.sync.dma_start(scatter_list[:], offs2)
 
         v_s_g = shared("v_s_g", [P, S], U8, "v_s_g")
         nc.vector.tensor_copy(v_s_g[:], tab_s[:].indirect(gather_list[:]))
         nc.vector.tensor_copy(staged[:, 2 * H : 2 * H + S].bitcast(I32), v_s_g[:].bitcast(I32))
-        for raw, c0 in ((wc8_s_raw, H), (wa4_s_raw, 0)):
-            nc.vector.tensor_copy(
-                staged[:, c0 : c0 + H].rearrange("p (b t m) -> p b t m", b=2, t=4),
-                raw[:].rearrange("p (b m t) -> p b t m", b=2, t=4),
-            )
+        nc.vector.tensor_copy(
+            staged[:, 0:H].rearrange("p (b t m) -> p b t m", b=2, t=4),
+            wa4_s_raw[:].rearrange("p (b m t) -> p b t m", b=2, t=4),
+        )
         for r in range(4):
             nc.sync.dma_start(planes[r:P:32, :].bitcast(I32), staged[8 * r : P : 32, :].bitcast(I32))
 
-        w_raw = shared("w_raw", [P, 3, 4, N], F32, "wa4_s_raw")
-        nc.sync.dma_start(w_raw[:, 2], wb_rows[:, :, 512:1024])
-        wd_raw = w_raw[:, 0:2]
-        for a in range(2):
-            nc.sync.dma_start(wd_raw[:, a], wd[512 * a : 512 * (a + 1), :].rearrange("(p j) c -> p j c", j=4))
-        wc8_raw = shared("wc8_raw", [P, 2, N], I32, "staged")
-        nc.sync.dma_start(wc8_raw[:], wc8_words.rearrange("a p c i -> p a (c i)").bitcast(I32))
+        wb_raw.append(shared("wb_raw1", [P, 4, 512], F32, "wa4_s_raw"))
+        nc.sync.dma_start(wb_raw[1][:], wb_rows[:, :, 512:1024])
 
         wa4 = held("wa4", [P, 2 * H], U8)
         nc.vector.tensor_copy(
@@ -110,7 +102,7 @@ def tile_list_profile_field_refresh_kernel(
                 copy(dst[:, m0:m1], src[:, m0:m1])
             return woven
 
-        mostly_scalar = [(nc.scalar.copy, 0, 96), (nc.vector.tensor_copy, 96, P)]
+        mostly_scalar = [(nc.scalar.copy, 0, 64), (nc.vector.tensor_copy, 64, P)]
         on_vector = [(nc.vector.tensor_copy, 0, P)]
         on_both = [(nc.scalar.copy, 0, P // 2), (nc.vector.tensor_copy, P // 2, P)]
 
@@ -121,19 +113,27 @@ def tile_list_profile_field_refresh_kernel(
             return codes, scales
 
         wbq = [quantise(cast_weight(mostly_scalar, wb_raw[0][:], "wb_bf0"), 512, "wbq0")]
-        pages[1] = shared("page1", [P, T2], F32, "wb_bf0")
-        nc.gpsimd.memset(pages[1][:], 0.0)
+        wd_raw = shared("wd_raw", [P, 2, 4, N], F32, "raw0")
+        for a in range(2):
+            nc.sync.dma_start(wd_raw[:, a], wd[512 * a : 512 * (a + 1), :].rearrange("(p j) c -> p j c", j=4))
+        wc8_raw = shared("wc8_raw", [P, 2, N], I32, "staged")
+        nc.sync.dma_start(wc8_raw[:], wc8_words.rearrange("a p c i -> p a (c i)").bitcast(I32))
         v_w = []
         for s, (j0, n) in enumerate(SLICES):
-            v_w.append(held("v_w%d" % s, [P, n], U32))
+            v_w.append(shared("v_w%d" % s, [P, n], U32, "wa4_raw" if s == 2 else "v_w%d" % s))
             nc.vector.tensor_copy(v_w[s][:], tab_w[:].indirect(gather_list[:, j0 // 16 : (j0 + n) // 16]))
 
-        late = shared("late", [P, S + 8], F32, "raw0")
+        late = shared("late", [P, S + 8], F32, "tab_w")
         wgo_sb = late[:, 0:S]
         bias = late[:, S : S + 4]
         nc.sync.dma_start(wgo_sb, wgo)
         nc.sync.dma_start(bias, bd.rearrange("(p i) -> p i", i=4))
-        wbq.append(quantise(cast_weight(on_vector, w_raw[:, 2], "wb_bf1"), 512, "wbq1"))
+        wbq.append(quantise(cast_weight(on_vector, wb_raw[1][:], "wb_bf1"), 512, "wbq1"))
+        wc8_s = shared("wc8_s", [P, H], U8, "wa4_s_raw")
+        nc.vector.tensor_copy(
+            wc8_s[:].rearrange("p (b t m) -> p b t m", b=2, t=4),
+            planes[:, H : 2 * H].rearrange("p (b m t) -> p b t m", b=2, t=4),
+        )
 
         def stage1(s, b):
             j0, n = SLICES[s]
@@ -157,7 +157,7 @@ def tile_list_profile_field_refresh_kernel(
                         start=True,
                         stop=True,
                     )
-                return bank[:].rearrange("p t n -> p n t")
+                return bank[:].rearrange("p t (n e) -> p n t e", e=2)
 
             def wa4_columns(t):
                 col = 512 * b + P * t
@@ -167,12 +167,12 @@ def tile_list_profile_field_refresh_kernel(
                 return wbq[b][0][:, P * t : P * (t + 1)], wbq[b][1][:, P * t : P * (t + 1)]
 
             def part(tile, c):
-                return tile[:, 512 * c : 512 * (c + 1)].rearrange("p (n t) -> p n t", t=4)
+                return tile[:, 512 * c : 512 * (c + 1)].rearrange("p (n e t) -> p n t e", e=2, t=4)
 
-            for c in range(n // P):
-                nc.scalar.copy(part(ha, c), product(c, FP4X4, wa4_columns))
-            for c in range(n // P):
-                nc.scalar.copy(part(hb, c), product(c, FP8X4, wb_columns))
+            kinds = [(ha, FP4X4, wa4_columns), (hb, FP8X4, wb_columns)]
+            for total, weight, columns in kinds[::-1] if b == 0 else kinds:
+                for c in range(n // P):
+                    nc.scalar.copy(part(total, c), product(c, weight, columns))
             nc.vector.tensor_tensor(h[:], ha[:], hb[:], ALU.max)
             hq[s, b] = quantise(h, n, "hq%d_%d" % (s, b))
 
@@ -253,7 +253,7 @@ def tile_list_profile_field_refresh_kernel(
             if step in halves:
                 stage1(*halves[step])
             if step == 0:
-                pages[3] = shared("page3", [P, T2], F32, "h11")
+                pages.append(shared("page3", [P, T2], F32, "h11"))
                 nc.gpsimd.memset(pages[3][:], 0.0)
             if step + 1 < len(order):
                 made.append(stage2(*order[step + 1], step + 1))

@@ -64,8 +64,10 @@ def tile_list_profile_field_refresh_kernel(
         nc.sync.dma_start(gather_list[:], offs)
         nc.sync.dma_start(tab_s[:].bitcast(I32), spread(tab_scales[0]))
         nc.sync.dma_start(wa4_s_raw[:].bitcast(I32), spread(wa4_scales[0]))
-        for a in range(2):
-            nc.sync.dma_start(staged[:, H + N * a : H + N * (a + 1)].bitcast(I32), spread(wc8_scales[a]))
+        nc.sync.dma_start(
+            staged[0:P:8, H : 2 * H].bitcast(I32).rearrange("q (a c) -> q a c", a=2),
+            wc8_scales.bitcast(I32).rearrange("a q c -> q a c"),
+        )
         wb_rows = wb.rearrange("(p j) c -> p j c", j=4)
         wb_raw = [shared("wb_raw0", [P, 4, 512], F32, "raw0")]
         nc.sync.dma_start(wb_raw[0][:], wb_rows[:, :, 0:512])
@@ -178,10 +180,10 @@ def tile_list_profile_field_refresh_kernel(
 
         hq = {}
         stage1(0, 0)
-        wdq = [quantise(cast_weight(on_vector, wd_raw[:, 0], "wd_bf0"), 512, "wdq0")]
+        wdq = [quantise(cast_weight(on_both, wd_raw[:, 0], "wd_bf0"), 512, "wdq0")]
         stage1(0, 1)
         stage1(1, 0)
-        wdq.append(quantise(cast_weight(on_both, wd_raw[:, 1], "wd_bf1"), 512, "wdq1"))
+        wdq.append(quantise(cast_weight(on_vector, wd_raw[:, 1], "wd_bf1"), 512, "wdq1"))
         wc8 = held("wc8", [P, 2 * N], U32)
         nc.vector.tensor_copy(
             wc8[:].rearrange("p (a i g m) -> p a g m i", a=2, i=4, m=4),
@@ -255,6 +257,7 @@ def tile_list_profile_field_refresh_kernel(
             if step == 0:
                 pages.append(shared("page3", [P, T2], F32, "h11"))
                 nc.gpsimd.memset(pages[3][:], 0.0)
-            if step + 1 < len(order):
-                made.append(stage2(*order[step + 1], step + 1))
+            ahead = 1 if step < 5 else 2
+            while len(made) < min(step + 1 + ahead, len(order)):
+                made.append(stage2(*order[len(made)], len(made)))
             scatter(s, i, *made[step])

@@ -47,16 +47,18 @@ def tile_list_profile_field_refresh_kernel(
 
         tab_s = held("tab_s", [P, T], U8)
         wa4_s_raw = shared("wa4_s_raw", [P, H], U8, "wa4_s_raw")
-        staged = shared("staged", [P, 2 * H + S], U8, "staged")
-        planes = held("planes", [P, 2 * H + S], U8)
+        staged = shared("staged", [P, H + S], U8, "staged")
+        planes = held("planes", [P, H + S], U8)
+        wc8_s_raw = held("wc8_s_raw", [P, N], U8)
         pages = [held("page%d" % i, [P, T2], F32) for i in range(3)]
         nc.gpsimd.memset(planes[:].bitcast(I32), 0)
+        nc.gpsimd.memset(wc8_s_raw[:].bitcast(I32), 0)
         nc.gpsimd.memset(pages[0][:], 0.0)
         nc.gpsimd.memset(pages[1][:], 0.0)
         nc.vector.memset(pages[2][:, 0 : T2 // 2 - 1], 0.0)
         nc.vector.memset(pages[2][:, T2 // 2 - 1 : T2], 0.0)
         w_s = planes[:, 0:H]
-        v_s = planes[:, 2 * H : 2 * H + S]
+        v_s = planes[:, H : H + S]
 
         def spread(rows):
             return rows.bitcast(I32).unsqueeze(1).to_broadcast([16, 8, rows.shape[1] // 4])
@@ -64,10 +66,6 @@ def tile_list_profile_field_refresh_kernel(
         nc.sync.dma_start(gather_list[:], offs)
         nc.sync.dma_start(tab_s[:].bitcast(I32), spread(tab_scales[0]))
         nc.sync.dma_start(wa4_s_raw[:].bitcast(I32), spread(wa4_scales[0]))
-        nc.sync.dma_start(
-            staged[0:P:8, H : 2 * H].bitcast(I32).rearrange("q (a c) -> q a c", a=2),
-            wc8_scales.bitcast(I32).rearrange("a q c -> q a c"),
-        )
         wb_rows = wb.rearrange("(p j) c -> p j c", j=4)
         wb_raw = [shared("wb_raw0", [P, 4, 512], F32, "raw0")]
         nc.sync.dma_start(wb_raw[0][:], wb_rows[:, :, 0:512])
@@ -76,10 +74,14 @@ def tile_list_profile_field_refresh_kernel(
         wa4_raw = shared("wa4_raw", [P, 2 * H], U8, "wa4_raw")
         nc.sync.dma_start(wa4_raw[:].bitcast(I32), wa4_words[0].bitcast(I32))
         nc.sync.dma_start(scatter_list[:], offs2)
+        for d in range(4):
+            nc.scalar.dma_start(
+                wc8_s_raw[32 * d : 32 * d + 8, :].bitcast(I32), wc8_scales[:, 4 * d : 4 * d + 4, :].bitcast(I32)
+            )
 
         v_s_g = shared("v_s_g", [P, S], U8, "v_s_g")
         nc.vector.tensor_copy(v_s_g[:], tab_s[:].indirect(gather_list[:]))
-        nc.vector.tensor_copy(staged[:, 2 * H : 2 * H + S].bitcast(I32), v_s_g[:].bitcast(I32))
+        nc.vector.tensor_copy(staged[:, H : H + S].bitcast(I32), v_s_g[:].bitcast(I32))
         nc.vector.tensor_copy(
             staged[:, 0:H].rearrange("p (b t m) -> p b t m", b=2, t=4),
             wa4_s_raw[:].rearrange("p (b m t) -> p b t m", b=2, t=4),
@@ -131,10 +133,10 @@ def tile_list_profile_field_refresh_kernel(
         nc.sync.dma_start(wgo_sb, wgo)
         nc.sync.dma_start(bias, bd.rearrange("(p i) -> p i", i=4))
         wbq.append(quantise(cast_weight(on_vector, wb_raw[1][:], "wb_bf1"), 512, "wbq1"))
-        wc8_s = shared("wc8_s", [P, H], U8, "wa4_s_raw")
+        wc8_s = shared("wc8_s", [P, N], U8, "wa4_s_raw")
         nc.vector.tensor_copy(
-            wc8_s[:].rearrange("p (b t m) -> p b t m", b=2, t=4),
-            planes[:, H : 2 * H].rearrange("p (b m t) -> p b t m", b=2, t=4),
+            wc8_s[:].rearrange("p (t m) -> p t m", t=4),
+            wc8_s_raw[:].rearrange("p (m t) -> p t m", t=4),
         )
 
         def stage1(s, b):
@@ -200,7 +202,7 @@ def tile_list_profile_field_refresh_kernel(
                 nc.tensor.matmul_mx(
                     out=yc[:],
                     lhsT=wc8[:, col : col + P].bitcast(FP8X4),
-                    lhsT_scale=wc8_s[:, col : col + P],
+                    lhsT_scale=wc8_s[4 * a : P, P * i : P * (i + 1)],
                     rhs=hq[s, a][0][:].bitcast(FP8X4),
                     rhs_scale=hq[s, a][1][:],
                     start=(a == 0),

@@ -248,7 +248,11 @@ def tile_list_profile_field_refresh_kernel(
             else:
                 nc.vector.tensor_tensor(places, y[:], gate[:], ALU.mult)
             if s == len(SLICES) - 1:
-                nc.sync.dma_start(out_rows[:, i, :], pages[i][:])
+                if i < 3:
+                    nc.sync.dma_start(out_rows[:, i, :], pages[i][:])
+                else:
+                    for queue, c0 in ((nc.sync, 0), (nc.scalar, T2 // 2)):
+                        queue.dma_start(out_rows[:, i, c0 : c0 + T2 // 2], pages[i][:, c0 : c0 + T2 // 2])
 
         order = [(s, i) for s in range(3) for i in range(4)]
         halves = {0: (1, 1), 1: (2, 0), 3: (2, 1)}

@@ -231,7 +231,7 @@ def tile_list_profile_field_refresh_kernel(
                 nc.vector.tensor_tensor(y[:], yc[:], weights, ALU.mult)
                 return y, gate
             half = ring.tile([P, n], F32, name="half", tag="half")
-            if step < 8:
+            if step < 7:
                 nc.vector.tensor_tensor(half[:], yc[:], weights, ALU.mult)
             else:
                 yc_sb = ring.tile([P, n], F32, name="yc_sb", tag="yc_sb")

@@ -45,20 +45,16 @@ def tile_list_profile_field_refresh_kernel(
         nc.vector.memset(warm[:], 0.0)
         nc.scalar.activation(warm_out[:], warm[:], ACT.Sigmoid)
 
-        tab_s = held("tab_s", [P, T], U8)
+        tab_s = shared("tab_s", [P, T], U8, "tab_s")
         wa4_s_raw = shared("wa4_s_raw", [P, H], U8, "wa4_s_raw")
         staged = shared("staged", [P, H + S], U8, "staged")
-        planes = held("planes", [P, H + S], U8)
         wc8_s_raw = held("wc8_s_raw", [P, N], U8)
         pages = [held("page%d" % i, [P, T2], F32) for i in range(3)]
-        nc.gpsimd.memset(planes[:].bitcast(I32), 0)
         nc.gpsimd.memset(wc8_s_raw[:].bitcast(I32), 0)
         nc.gpsimd.memset(pages[0][:], 0.0)
         nc.gpsimd.memset(pages[1][:], 0.0)
         nc.vector.memset(pages[2][:, 0 : T2 // 2 - 1], 0.0)
         nc.vector.memset(pages[2][:, T2 // 2 - 1 : T2], 0.0)
-        w_s = planes[:, 0:H]
-        v_s = planes[:, H : H + S]
 
         def spread(rows):
             return rows.bitcast(I32).unsqueeze(1).to_broadcast([16, 8, rows.shape[1] // 4])
@@ -86,6 +82,9 @@ def tile_list_profile_field_refresh_kernel(
             staged[:, 0:H].rearrange("p (b t m) -> p b t m", b=2, t=4),
             wa4_s_raw[:].rearrange("p (b m t) -> p b t m", b=2, t=4),
         )
+        planes = shared("planes", [P, H + S], U8, "tab_s")
+        w_s = planes[:, 0:H]
+        v_s = planes[:, H : H + S]
         for r in range(4):
             nc.sync.dma_start(planes[r:P:32, :].bitcast(I32), staged[8 * r : P : 32, :].bitcast(I32))
 

@@ -225,7 +225,8 @@ def tile_list_profile_field_refresh_kernel(
                 gate = ring3.tile([P, n], F32, name="gate", tag="gate")
             nc.scalar.activation(gate[:], yd[:], ACT.Sigmoid, bias=bias[:, i : i + 1])
 
-            y = ring3.tile([P, n], F32, name="y", tag="ysb")
+            if step < 11:
+                y = ring3.tile([P, n], F32, name="y", tag="ysb")
             if step < 5:
                 nc.vector.tensor_tensor(y[:], yc[:], weights, ALU.mult)
                 return y, gate
@@ -236,6 +237,8 @@ def tile_list_profile_field_refresh_kernel(
                 yc_sb = ring.tile([P, n], F32, name="yc_sb", tag="yc_sb")
                 nc.scalar.copy(yc_sb[:], yc[:])
                 nc.gpsimd.tensor_tensor(half[:], yc_sb[:], weights, ALU.mult)
+            if step == 11:
+                return half, gate
             [nc.gpsimd, nc.vector][step == 5].tensor_tensor(y[:], half[:], gate[:], ALU.mult)
             return y, None
 

from contextlib import ExitStack

import concourse.mybir as mybir

K, H, N, T, S, T2 = 512, 1024, 512, 2048, 1024, 2048
FLOPS = 4 * K * H * S + 4 * H * N * S

F32 = mybir.dt.float32
BF16 = mybir.dt.bfloat16
I32 = mybir.dt.int32
U32 = mybir.dt.uint32
U16 = mybir.dt.uint16
U8 = mybir.dt.uint8
FP8X4 = mybir.dt.float8_e4m3fn_x4
FP4X4 = mybir.dt.float4_e2m1fn_x4
ALU = mybir.AluOpType
ACT = mybir.ActivationFunctionType

P = 128
SLICES = [(0, 256), (256, 256), (512, 512)]


def tile_list_profile_field_refresh_kernel(
    tc, tab_words, tab_scales, offs, wa4_words, wa4_scales, wb, wc8_words, wc8_scales, wd, bd, wgo, offs2, out
):
    nc = tc.nc
    with ExitStack() as ctx:
        keep = ctx.enter_context(tc.tile_pool(name="keep", bufs=1))
        ring = ctx.enter_context(tc.tile_pool(name="ring", bufs=2))
        ring3 = ctx.enter_context(tc.tile_pool(name="ring3", bufs=3))
        ps1 = ctx.enter_context(tc.psum_pool(name="ps1", bufs=4))
        ps2 = ctx.enter_context(tc.psum_pool(name="ps2", bufs=4))

        def held(name, shape, dtype):
            return keep.tile(shape, dtype, name=name, align_bytes=64)

        gather_list = keep.tile([P, S // 16], U16, name="gather_list")
        scatter_list = keep.tile([P, S // 16], U16, name="scatter_list")

        def shared(name, shape, dtype, tag):
            return keep.tile(shape, dtype, name=name, tag=tag, align_bytes=64)

        warm = held("warm", [P, 1], F32)
        warm_out = held("warm_out", [P, 1], F32)
        nc.vector.memset(warm[:], 0.0)
        nc.scalar.activation(warm_out[:], warm[:], ACT.Sigmoid)

        tab_s = shared("tab_s", [P, T], U8, "tab_s")
        wa4_s_raw = shared("wa4_s_raw", [P, H], U8, "wa4_s_raw")
        staged = shared("staged", [P, H + S], U8, "staged")
        wc8_s_raw = held("wc8_s_raw", [P, N], U8)
        pages = [held("page%d" % i, [P, T2], F32) for i in range(3)]
        nc.gpsimd.memset(wc8_s_raw[:].bitcast(I32), 0)
        nc.gpsimd.memset(pages[0][:], 0.0)
        nc.gpsimd.memset(pages[1][:], 0.0)
        nc.vector.memset(pages[2][:, 0 : T2 // 2 - 1], 0.0)
        nc.vector.memset(pages[2][:, T2 // 2 - 1 : T2], 0.0)

        def spread(rows):
            return rows.bitcast(I32).unsqueeze(1).to_broadcast([16, 8, rows.shape[1] // 4])

        nc.sync.dma_start(gather_list[:], offs)
        nc.sync.dma_start(tab_s[:].bitcast(I32), spread(tab_scales[0]))
        nc.sync.dma_start(wa4_s_raw[:].bitcast(I32), spread(wa4_scales[0]))
        wb_rows = wb.rearrange("(p j) c -> p j c", j=4)
        wb_raw = [shared("wb_raw0", [P, 4, 512], F32, "raw0")]
        nc.sync.dma_start(wb_raw[0][:], wb_rows[:, :, 0:512])
        tab_w = shared("tab_w", [P, T], U32, "tab_w")
        nc.sync.dma_start(tab_w[:].bitcast(I32), tab_words[0].rearrange("p t i -> p (t i)").bitcast(I32))
        wa4_raw = shared("wa4_raw", [P, 2 * H], U8, "wa4_raw")
        nc.sync.dma_start(wa4_raw[:].bitcast(I32), wa4_words[0].bitcast(I32))
        nc.sync.dma_start(scatter_list[:], offs2)
        for d in range(4):
            nc.scalar.dma_start(
                wc8_s_raw[32 * d : 32 * d + 8, :].bitcast(I32), wc8_scales[:, 4 * d : 4 * d + 4, :].bitcast(I32)
            )

        v_s_g = shared("v_s_g", [P, S], U8, "v_s_g")
        nc.vector.tensor_copy(v_s_g[:], tab_s[:].indirect(gather_list[:]))
        nc.vector.tensor_copy(staged[:, H : H + S].bitcast(I32), v_s_g[:].bitcast(I32))
        nc.vector.tensor_copy(
            staged[:, 0:H].rearrange("p (b t m) -> p b t m", b=2, t=4),
            wa4_s_raw[:].rearrange("p (b m t) -> p b t m", b=2, t=4),
        )
        planes = shared("planes", [P, H + S], U8, "tab_s")
        w_s = planes[:, 0:H]
        v_s = planes[:, H : H + S]
        for r in range(4):
            nc.sync.dma_start(planes[r:P:32, :].bitcast(I32), staged[8 * r : P : 32, :].bitcast(I32))

        wb_raw.append(shared("wb_raw1", [P, 4, 512], F32, "wa4_s_raw"))
        nc.sync.dma_start(wb_raw[1][:], wb_rows[:, :, 512:1024])

        wa4 = held("wa4", [P, 2 * H], U8)
        nc.vector.tensor_copy(
            wa4[:].bitcast(U16).rearrange("p (b t m) -> p b t m", b=2, t=4),
            wa4_raw[:].bitcast(U16).rearrange("p (b m t) -> p b t m", b=2, t=4),
        )

        def cast_weight(shares, raw, name):
            woven = shared(name, [P, 2048], BF16, name)
            dst = woven[:].rearrange("p (t m j) -> p m j t", t=4, j=4)
            src = raw.rearrange("p j (m t) -> p m j t", t=4)
            for copy, m0, m1 in shares:
                copy(dst[:, m0:m1], src[:, m0:m1])
            return woven

        mostly_scalar = [(nc.scalar.copy, 0, 64), (nc.vector.tensor_copy, 64, P)]
        on_vector = [(nc.vector.tensor_copy, 0, P)]
        on_both = [(nc.scalar.copy, 0, P // 2), (nc.vector.tensor_copy, P // 2, P)]

        def quantise(woven, width, name):
            codes = held(name + "_w", [P, width], U32)
            scales = held(name + "_s", [P, width], U8)
            nc.vector.quantize_mx(out=codes[:].bitcast(FP8X4), scales=scales[:], in_=woven[:])
            return codes, scales

        wbq = [quantise(cast_weight(mostly_scalar, wb_raw[0][:], "wb_bf0"), 512, "wbq0")]
        wd_raw = shared("wd_raw", [P, 2, 4, N], F32, "raw0")
        for a in range(2):
            nc.sync.dma_start(wd_raw[:, a], wd[512 * a : 512 * (a + 1), :].rearrange("(p j) c -> p j c", j=4))
        wc8_raw = shared("wc8_raw", [P, 2, N], I32, "staged")
        nc.sync.dma_start(wc8_raw[:], wc8_words.rearrange("a p c i -> p a (c i)").bitcast(I32))
        v_w = []
        for s, (j0, n) in enumerate(SLICES):
            v_w.append(shared("v_w%d" % s, [P, n], U32, "wa4_raw" if s == 2 else "v_w%d" % s))
            nc.vector.tensor_copy(v_w[s][:], tab_w[:].indirect(gather_list[:, j0 // 16 : (j0 + n) // 16]))

        late = shared("late", [P, S + 8], F32, "tab_w")
        wgo_sb = late[:, 0:S]
        bias = late[:, S : S + 4]
        nc.sync.dma_start(wgo_sb, wgo)
        nc.sync.dma_start(bias, bd.rearrange("(p i) -> p i", i=4))
        wbq.append(quantise(cast_weight(on_vector, wb_raw[1][:], "wb_bf1"), 512, "wbq1"))
        wc8_s = shared("wc8_s", [P, N], U8, "wa4_s_raw")
        nc.vector.tensor_copy(
            wc8_s[:].rearrange("p (t m) -> p t m", t=4),
            wc8_s_raw[:].rearrange("p (m t) -> p t m", t=4),
        )

        def stage1(s, b):
            j0, n = SLICES[s]
            if (s, b) == (1, 1):
                h = shared("h11", [P, 4 * n], BF16, "h11")
            else:
                h = ring.tile([P, 4 * n], BF16, name="h", tag="h", align_bytes=64)
            ha = ring.tile([P, 4 * n], BF16, name="ha", tag="ha", align_bytes=64)
            hb = ring.tile([P, 4 * n], BF16, name="hb", tag="hb", align_bytes=64)

            def product(c, weight, columns):
                bank = ps1.tile([P, 4, P], F32, name="bank", tag="bank")
                for t in range(4):
                    codes, scales = columns(t)
                    nc.tensor.matmul_mx(
                        out=bank[:, t, :],
                        lhsT=codes.bitcast(weight),
                        lhsT_scale=scales,
                        rhs=v_w[s][:, c * P : (c + 1) * P].bitcast(FP8X4),
                        rhs_scale=v_s[:, j0 + c * P : j0 + (c + 1) * P],
                        start=True,
                        stop=True,
                    )
                return bank[:].rearrange("p t (n e) -> p n t e", e=2)

            def wa4_columns(t):
                col = 512 * b + P * t
                return wa4[:, 2 * col : 2 * (col + P)], w_s[:, col : col + P]

            def wb_columns(t):
                return wbq[b][0][:, P * t : P * (t + 1)], wbq[b][1][:, P * t : P * (t + 1)]

            def part(tile, c):
                return tile[:, 512 * c : 512 * (c + 1)].rearrange("p (n e t) -> p n t e", e=2, t=4)

            kinds = [(ha, FP4X4, wa4_columns), (hb, FP8X4, wb_columns)]
            for total, weight, columns in kinds[::-1] if b == 0 else kinds:
                for c in range(n // P):
                    nc.scalar.copy(part(total, c), product(c, weight, columns))
            nc.vector.tensor_tensor(h[:], ha[:], hb[:], ALU.max)
            hq[s, b] = quantise(h, n, "hq%d_%d" % (s, b))

        hq = {}
        stage1(0, 0)
        wdq = [quantise(cast_weight(on_both, wd_raw[:, 0], "wd_bf0"), 512, "wdq0")]
        stage1(0, 1)
        stage1(1, 0)
        wdq.append(quantise(cast_weight(on_vector, wd_raw[:, 1], "wd_bf1"), 512, "wdq1"))
        wc8 = held("wc8", [P, 2 * N], U32)
        nc.vector.tensor_copy(
            wc8[:].rearrange("p (a i g m) -> p a g m i", a=2, i=4, m=4),
            wc8_raw[:].bitcast(U32).rearrange("p a (g m i) -> p a g m i", i=4, m=4),
        )

        out_rows = out.rearrange("(p i) t -> p i t", i=4)

        def stage2(s, i, step):
            j0, n = SLICES[s]
            yc = ps2.tile([P, n], F32, name="yc", tag="y")
            for a in range(2):
                col = N * a + P * i
                nc.tensor.matmul_mx(
                    out=yc[:],
                    lhsT=wc8[:, col : col + P].bitcast(FP8X4),
                    lhsT_scale=wc8_s[4 * a : P, P * i : P * (i + 1)],
                    rhs=hq[s, a][0][:].bitcast(FP8X4),
                    rhs_scale=hq[s, a][1][:],
                    start=(a == 0),
                    stop=(a == 1),
                )
            yd = ps2.tile([P, n], F32, name="yd", tag="y")
            for a in range(2):
                nc.tensor.matmul_mx(
                    out=yd[:],
                    lhsT=wdq[a][0][:, P * i : P * (i + 1)].bitcast(FP8X4),
                    lhsT_scale=wdq[a][1][:, P * i : P * (i + 1)],
                    rhs=hq[s, a][0][:].bitcast(FP8X4),
                    rhs_scale=hq[s, a][1][:],
                    start=(a == 0),
                    stop=(a == 1),
                )
            weights = wgo_sb[:, j0 : j0 + n]
            if step == 5:
                gate = ring.tile([P, n], F32, name="gate", tag="half")
            else:
                gate = ring3.tile([P, n], F32, name="gate", tag="gate")
            nc.scalar.activation(gate[:], yd[:], ACT.Sigmoid, bias=bias[:, i : i + 1])

            if step < 11:
                y = ring3.tile([P, n], F32, name="y", tag="ysb")
            if step < 5:
                nc.vector.tensor_tensor(y[:], yc[:], weights, ALU.mult)
                return y, gate
            half = ring.tile([P, n], F32, name="half", tag="half")
            if step < 7:
                nc.vector.tensor_tensor(half[:], yc[:], weights, ALU.mult)
            else:
                yc_sb = ring.tile([P, n], F32, name="yc_sb", tag="yc_sb")
                nc.scalar.copy(yc_sb[:], yc[:])
                nc.gpsimd.tensor_tensor(half[:], yc_sb[:], weights, ALU.mult)
            if step == 11:
                return half, gate
            [nc.gpsimd, nc.vector][step == 5].tensor_tensor(y[:], half[:], gate[:], ALU.mult)
            return y, None

        def scatter(s, i, y, gate):
            j0, n = SLICES[s]
            places = pages[i][:].indirect(scatter_list[:, j0 // 16 : (j0 + n) // 16])
            if gate is None:
                nc.vector.tensor_copy(places, y[:])
            else:
                nc.vector.tensor_tensor(places, y[:], gate[:], ALU.mult)
            if s == len(SLICES) - 1:
                if i < 3:
                    nc.sync.dma_start(out_rows[:, i, :], pages[i][:])
                else:
                    for queue, c0 in ((nc.sync, 0), (nc.scalar, T2 // 2)):
                        queue.dma_start(out_rows[:, i, c0 : c0 + T2 // 2], pages[i][:, c0 : c0 + T2 // 2])

        order = [(s, i) for s in range(3) for i in range(4)]
        halves = {0: (1, 1), 1: (2, 0), 3: (2, 1)}
        made = [stage2(0, 0, 0)]
        for step, (s, i) in enumerate(order):
            if step in halves:
                stage1(*halves[step])
            if step == 0:
                pages.append(shared("page3", [P, T2], F32, "h11"))
                nc.gpsimd.memset(pages[3][:], 0.0)
            ahead = 1 if step < 5 else 2
            while len(made) < min(step + 1 + ahead, len(order)):
                made.append(stage2(*order[len(made)], len(made)))
            scatter(s, i, *made[step])
